import numpy as np
import ml_dtypes


def mxq(x, axis, fmt="e4m3"):
    dtype, down = {"e4m3": (ml_dtypes.float8_e4m3fn, 7), "e5m2": (ml_dtypes.float8_e5m2, 14)}[fmt]
    v = np.moveaxis(np.asarray(x, np.float32).astype(ml_dtypes.bfloat16).astype(np.float64), axis, -1)
    blocks = v.reshape(v.shape[:-1] + (-1, 32))
    amax = np.abs(blocks).max(-1, keepdims=True)
    byte = np.maximum(np.where(amax > 0, np.frexp(amax)[1] - 1 + 127, 0) - down, 1)
    scale = np.exp2(byte - 127.0)
    codes = (blocks / scale).astype(np.float32).astype(dtype).astype(np.float64)
    return np.moveaxis((codes * scale).reshape(v.shape), -1, axis)


WIDE = False


def mx_kscale(k):
    if not WIDE:
        return np.ones(k)
    levels = np.array([10, -10, 5, -5, 0])
    if k % 512:
        return np.exp2(np.random.permutation(np.resize(levels, k // 32))).repeat(32)
    a = np.empty((k // 512, 16))
    for p in range(k // 512):
        a[p, :8] = np.random.permutation(np.resize(levels, 8))
        for g in range(8):
            far = levels[np.abs(levels - a[p, g]) >= 10]
            a[p, g + 8] = far[np.random.randint(len(far))]
    return np.exp2(a.ravel()).repeat(32)


BF16 = ml_dtypes.bfloat16


def bf(x):
    return np.asarray(x, np.float32).astype(BF16)


def f64(x):
    return np.asarray(x).astype(np.float64)


T, D, E, R = 1024, 1024, 4, 256
ER = E * R


def draw0():
    s, t = mx_kscale(D), mx_kscale(ER).reshape(E, R)
    x0 = bf(np.random.standard_normal((T, D)) * s)
    x = bf(np.random.standard_normal((T, D)) * s)
    v = bf(np.random.standard_normal((D, E, R)) / np.sqrt(D) / s[:, None, None])
    wg = bf(np.random.standard_normal((D, E)) / np.sqrt(D) / s[:, None])
    c = bf((1.0 + 0.1 * np.random.standard_normal((E, R))) * t)
    u = bf(np.random.standard_normal((E, R, D)) * 2.0 / np.sqrt(R) / t[:, :, None])
    b = bf(0.3 * np.random.standard_normal(D) * np.ones(D))
    return {"x0": x0, "x": x, "v": v, "wg": wg, "c": c, "u": u, "b": b}


def core(x0, x, v, wg, c, u, b):
    x0, x, v, wg, c, u, b = f64(x0), f64(x), f64(v), f64(wg), f64(c), f64(u), f64(b)
    t, d = x.shape
    e, r = c.shape
    p = (mxq(x, 1, "e4m3") @ mxq(v.reshape(d, e * r), 0, "e4m3")).reshape(t, e, r)
    a = np.stack([np.sum(x * wg[:, i], axis=1) for i in range(e)], axis=1)
    g = np.exp(a - a.max(axis=-1, keepdims=True))
    g = g / g.sum(axis=-1, keepdims=True)
    h = g[:, :, None] * np.tanh(p) * c[None, :, :]
    z = mxq(h.reshape(t, e * r), 1, "e4m3") @ mxq(u.reshape(e * r, d), 0, "e4m3")
    return x0 * (z + b[None, :]) + x


def e4m3fn_bytes(y):
    return np.clip(np.asarray(y, np.float64), -448.0, 448.0).astype(np.float32).astype(ml_dtypes.float8_e4m3fn).view(np.uint8)


def e4m3fn_values(b):
    return np.asarray(b, np.uint8).view(ml_dtypes.float8_e4m3fn).astype(np.float64)


def setup_inputs():
    d = draw0()
    x0 = np.asarray(d['v']).astype(np.float64)
    s = (np.max(np.abs(x0), axis=(1, 2), keepdims=True) / 448.0).astype(np.float32)
    out = {}
    for k, v in d.items():
        if k == 'v':
            out['v_bytes'] = e4m3fn_bytes(x0 / s.astype(np.float64))
            out['v_scale'] = s
        else:
            out[k] = v
    return out


def reference(x0, x, v_bytes, v_scale, wg, c, u, b):
    return core(x0, x, e4m3fn_values(v_bytes) * v_scale.astype(np.float64), wg, c, u, b)

@@ -1,0 +1,462 @@
+from contextlib import ExitStack
+
+import concourse.mybir as mybir
+from concourse.masks import make_identity
+
+T, D, E, R = 1024, 1024, 4, 256
+FLOPS = 2 * T * D * E * R * 2 + 2 * T * D * E
+
+F32 = mybir.dt.float32
+BF16 = mybir.dt.bfloat16
+U32 = mybir.dt.uint32
+U8 = mybir.dt.uint8
+FP8 = mybir.dt.float8_e4m3fn
+FP8X4 = mybir.dt.float8_e4m3fn_x4
+ALU = mybir.AluOpType
+ACT = mybir.ActivationFunctionType
+
+P = 128
+TILES = T // P
+GATE_BATCHES = ((0, 1), (2, 3, 4, 5, 6, 7))
+GATE_COLS = 16
+TURNED = True
+ADD_G = 768
+LAG = 2
+U11 = "V"
+
+
+def tile_dcnmixlowrankcrossexperts_kernel(tc, x0, x, v_bytes, v_scale, wg, c, u, b, out):
+    nc = tc.nc
+    with ExitStack() as ctx:
+        keep = ctx.enter_context(tc.tile_pool(name="keep", bufs=1))
+        work = ctx.enter_context(tc.tile_pool(name="work", bufs=3))
+        psum = ctx.enter_context(tc.psum_pool(name="psum", bufs=2))
+        ctx.enter_context(tc.manual_schedule())
+
+        def kept(name, shape, dtype):
+            return keep.tile(shape, dtype, name=name, align_bytes=64)
+
+        ident32 = kept("ident32", [P, P], F32)
+        ident16 = kept("ident16", [P, P], BF16)
+        vscale = kept("vscale", [P, 2, 4], F32)
+        wg_sb = kept("wg_sb", [P, 2, 4, E], BF16)
+        c_rows = kept("c_rows", [P, E * R], BF16)
+        c_sel = kept("c_sel", [P, 2, 4, P], BF16)
+        b_row = kept("b_row", [P, D], BF16)
+        b_all = kept("b_all", [P, D], BF16)
+        warm = kept("warm", [P, 2], F32)
+        v_raw = [kept("v_raw%d" % g, [P, 4, E * R], U8) for g in range(2)]
+        v_wide = {(g, h): kept("v_wide%d%d" % (g, h), [P, 4, 512], BF16) for g in range(2) for h in range(2)}
+        v_grouped = {(g, h): kept("v_grouped%d%d" % (g, h), [P, 2048], BF16) for g in range(2) for h in range(2)}
+        v_codes = {(g, h): kept("v_codes%d%d" % (g, h), [P, 512], U32) for g in range(2) for h in range(2)}
+        v_scales = {(g, h): kept("v_scales%d%d" % (g, h), [P, 512], U8) for g in range(2) for h in range(2)}
+        u_raw = [kept("u_raw%d" % h, [P, 4, D], BF16) for h in range(2)]
+        u_grouped = {(h, s): kept("u_grouped%d%d" % (h, s), [P, 2048], BF16) for h in range(2) for s in range(2)}
+        u_codes = {(h, s): kept("u_codes%d%d" % (h, s), [P, 512], U32) for h in range(2) for s in range(2)}
+        u_scales = {(h, s): kept("u_scales%d%d" % (h, s), [P, 512], U8) for h in range(2) for s in range(2)}
+        x_sb = [kept("x_sb%d" % j, [P, D], BF16) for j in range(TILES)]
+        x0_sb = [kept("x0_sb%d" % j, [P, D], BF16) for j in range(TILES)]
+        x_grouped = [kept("x_grouped%d" % j, [P, 2, P, 4], BF16) for j in range(TILES)]
+        x_codes = [kept("x_codes%d" % j, [P, 2 * P], U32) for j in range(TILES)]
+        x_scales = [kept("x_scales%d" % j, [P, 2 * P], U8) for j in range(TILES)]
+        h_grouped = [kept("h_grouped%d" % j, [P, 2, P, 4], BF16) for j in range(TILES)]
+        h_codes = [kept("h_codes%d" % j, [P, 2 * P], U32) for j in range(TILES)]
+        h_scales = [kept("h_scales%d" % j, [P, 2 * P], U8) for j in range(TILES)]
+        batches = len(GATE_BATCHES)
+        batch_of = {j: (q, jj) for q in range(batches) for jj, j in enumerate(GATE_BATCHES[q])}
+        gate_parts = [kept("gate_parts%d" % q, [P, (len(GATE_BATCHES[q]) - 1) * GATE_COLS + P], BF16) for q in range(batches)]
+        gate_rows = [kept("gate_rows%d" % q, [P, len(GATE_BATCHES[q]), P], BF16) for q in range(batches)]
+        gate_tmp = [{n: kept("gate_%s%d" % (n, q), [P, len(GATE_BATCHES[q]), w], F32)
+                     for n, w in (("max", 1), ("diff", E), ("exp", E), ("sum", 1), ("inv", 1), ("g", E), ("rest", E))}
+                    for q in range(batches)]
+        b_col = kept("b_col", [P, 4, 2], F32)
+        banks = {}
+
+        def shared_bank(name, shape, dtype):
+            return psum.tile(shape, dtype, name=name, tag="shared", bufs=4)
+
+        nc.scalar.dma_start(out=vscale[:], in_=v_scale.rearrange("(g p t) a o -> p g (t a o)", p=P, t=4))
+        nc.scalar.dma_start(out=wg_sb[:].rearrange("p g t e -> p g (t e)"), in_=wg.rearrange("(g p t) e -> p g (t e)", p=P, t=4))
+        nc.vector.memset(warm[:], 0.0)
+        nc.scalar.activation(out=warm[:, 1:2], in_=warm[:, 0:1], func=ACT.Exp)
+        nc.vector.memset(c_rows[:], 0.0)
+        nc.vector.memset(b_row[:], 0.0)
+        for q in range(batches):
+            nc.vector.memset(gate_parts[q][:], 0.0)
+        make_identity(nc, ident32[:])
+        make_identity(nc, ident16[:])
+
+        v_rows = v_bytes.rearrange("(g p t) e r -> g p (t e r)", p=P, t=4)
+        u_rows = u.rearrange("e r d -> (e r) d").rearrange("(h q t i) d -> h t q i d", h=2, t=4, i=4)
+
+        def load_x(j):
+            nc.sync.dma_start(out=x_sb[j][:], in_=x[j * P:(j + 1) * P, :])
+
+        nc.sync.dma_start(out=v_raw[0][:].rearrange("p t n -> p (t n)"), in_=v_rows[0])
+        load_x(0)
+        load_x(1)
+        nc.sync.dma_start(out=v_raw[1][:].rearrange("p t n -> p (t n)"), in_=v_rows[1])
+        load_x(2)
+        load_x(3)
+        for e in range(E):
+            nc.sync.dma_start(out=c_rows[4 * e:4 * e + 4, e * R:(e + 1) * R], in_=c[e].partition_broadcast(4))
+        nc.sync.dma_start(out=b_row[0:1, :], in_=b.rearrange("(o d) -> o d", o=1))
+        for j in range(4, TILES):
+            load_x(j)
+        for h in range(2):
+            for t in range(4):
+                nc.sync.dma_start(out=u_raw[h][:, t, :], in_=u_rows[h][t])
+        for j in range(TILES):
+            nc.sync.dma_start(out=x0_sb[j][:], in_=x0[j * P:(j + 1) * P, :])
+
+        def copy_on(engine, out_ap, in_ap):
+            if engine == "V":
+                nc.vector.tensor_copy(out=out_ap, in_=in_ap)
+            else:
+                nc.scalar.copy(out=out_ap, in_=in_ap)
+
+        def quantize(codes, scales, grouped):
+            nc.vector.quantize_mx(out=codes.bitcast(FP8X4), scales=scales, in_=grouped)
+
+        def widen_v(engine, g, h, slots=range(4)):
+            for t in slots:
+                src = v_raw[g][:, t, 512 * h:512 * (h + 1)].bitcast(FP8)
+                if engine == "V":
+                    nc.vector.tensor_scalar(out=v_wide[g, h][:, t, :], in0=src, scalar1=vscale[:, g, t:t + 1],
+                                            scalar2=None, op0=ALU.mult)
+                else:
+                    nc.scalar.activation(out=v_wide[g, h][:, t, :], in_=src, func=ACT.Copy, scale=vscale[:, g, t:t + 1])
+
+        def group_v(engine, g, h):
+            copy_on(engine, v_grouped[g, h][:].rearrange("p (s q i t) -> p s q t i", s=4, i=4, t=4),
+                    v_wide[g, h][:].rearrange("p t (q s i) -> p s q t i", s=4, i=4))
+
+        def quantize_v(g, h):
+            quantize(v_codes[g, h][:], v_scales[g, h][:], v_grouped[g, h][:])
+
+        def group_u(engine, h, s):
+            copy_on(engine, u_grouped[h, s][:].rearrange("p (q i t) -> p q t i", i=4, t=4),
+                    u_raw[h][:, :, 512 * s:512 * (s + 1)].rearrange("p t (q i) -> p q t i", i=4))
+
+        def quantize_u(h, s):
+            quantize(u_codes[h, s][:], u_scales[h, s][:], u_grouped[h, s][:])
+
+        def turn_x(j):
+            bank = shared_bank("xt%d" % j, [P, 4, P], F32)
+            words = x_sb[j][:].bitcast(F32)
+            for g in range(2):
+                for w in range(2):
+                    nc.tensor.transpose(bank[:, 2 * g + w, :], words[:, 256 * g + w:256 * (g + 1):2], ident32[:])
+            banks["xt", j] = bank
+
+        def empty_x(j):
+            words = x_grouped[j][:].rearrange("p g n t -> p (g n t)").bitcast(F32)
+            nc.scalar.copy(out=words.rearrange("p (g n w) -> p g n w", g=2, w=2),
+                           in_=banks["xt", j][:].rearrange("p (g w) n -> p g n w", g=2))
+
+        def quantize_x(j):
+            quantize(x_codes[j][:], x_scales[j][:], x_grouped[j][:].rearrange("p g n t -> p (g n t)"))
+
+        def gate_logits(j):
+            q, jj = batch_of[j]
+            if jj == 0:
+                banks["a", q] = shared_bank("logits%d" % q, [P, len(GATE_BATCHES[q]), E], F32)
+            for g in range(2):
+                for t in range(4):
+                    nc.tensor.matmul(banks["a", q][:, jj, :], lhsT=x_grouped[j][:, g, :, t], rhs=wg_sb[:, g, t, :],
+                                     start=(g == 0 and t == 0), stop=(g == 1 and t == 3))
+
+        def softmax_steps(q):
+            a = banks["a", q]
+            tmp = gate_tmp[q]
+            wide = [P, len(GATE_BATCHES[q]), E]
+            parts = gate_parts[q][:, 0:len(GATE_BATCHES[q]) * GATE_COLS].rearrange("p (j e s) -> p j e s", e=E, s=4)
+            return [
+                lambda: nc.vector.tensor_reduce(out=tmp["max"][:, :, 0], in_=a[:], axis=mybir.AxisListType.X, op=ALU.max),
+                lambda: nc.vector.tensor_tensor(out=tmp["diff"][:], in0=a[:], in1=tmp["max"][:].to_broadcast(wide), op=ALU.subtract),
+                lambda: nc.scalar.activation(out=tmp["exp"][:], in_=tmp["diff"][:], func=ACT.Exp),
+                lambda: nc.vector.tensor_reduce(out=tmp["sum"][:, :, 0], in_=tmp["exp"][:], axis=mybir.AxisListType.X, op=ALU.add),
+                lambda: nc.vector.reciprocal(out=tmp["inv"][:], in_=tmp["sum"][:]),
+                lambda: nc.vector.tensor_tensor(out=tmp["g"][:], in0=tmp["exp"][:], in1=tmp["inv"][:].to_broadcast(wide), op=ALU.mult),
+                lambda: nc.vector.tensor_copy(out=parts[:, :, :, 0], in_=tmp["g"][:]),
+                lambda: nc.vector.tensor_tensor(out=tmp["rest"][:], in0=tmp["g"][:], in1=parts[:, :, :, 0], op=ALU.subtract),
+                lambda: nc.vector.tensor_copy(out=parts[:, :, :, 1], in_=tmp["rest"][:]),
+                lambda: nc.vector.tensor_tensor(out=parts[:, :, :, 2], in0=tmp["rest"][:], in1=parts[:, :, :, 1], op=ALU.subtract),
+            ]
+
+        def turn_gate(q):
+            bank = shared_bank("gate_t%d" % q, [P, len(GATE_BATCHES[q]), P], BF16)
+            for jj in range(len(GATE_BATCHES[q])):
+                nc.tensor.transpose(bank[:, jj, :], gate_parts[q][:, jj * GATE_COLS:jj * GATE_COLS + P], ident16[:])
+            nc.scalar.copy(out=gate_rows[q][:], in_=bank[:])
+
+        def select_c():
+            nc.vector.tensor_copy(out=c_sel[:].rearrange("p h s (q i) -> p h s q i", i=4),
+                                  in_=c_rows[:].rearrange("p (h q s i) -> p h s q i", h=2, s=4, i=4))
+
+        def spread_b():
+            bank = shared_bank("b_bank", [P, D], BF16)
+            for s in range(2):
+                nc.tensor.matmul(bank[:, 512 * s:512 * (s + 1)], lhsT=ident16[:, 0:1].to_broadcast([P, P]),
+                                 rhs=b_row[:, 512 * s:512 * (s + 1)], start=True, stop=True)
+            nc.scalar.copy(out=b_all[:], in_=bank[:])
+
+        def project_down(j, h):
+            bank = psum.tile([P, 4, P], F32, name="p%d%d" % (j, h), tag="p")
+            for s in range(4):
+                cols = slice(P * s, P * (s + 1))
+                for g in range(2):
+                    nc.tensor.matmul_mx(out=bank[:, s, :], lhsT=v_codes[g, h][:, cols].bitcast(FP8X4),
+                                        lhsT_scale=v_scales[g, h][:, cols],
+                                        rhs=x_codes[j][:, P * g:P * (g + 1)].bitcast(FP8X4),
+                                        rhs_scale=x_scales[j][:, P * g:P * (g + 1)], start=(g == 0), stop=(g == 1))
+            banks["p", j, h] = bank
+
+        def tanh_p(j, h):
+            th = work.tile([P, P, 4], F32, name="tanh%d%d" % (j, h), tag="tanh", bufs=4)
+            nc.scalar.activation(out=th[:], in_=banks["p", j, h][:].rearrange("p s n -> p n s"), func=ACT.Tanh)
+            banks["th", j, h] = th
+
+        def gate_times_c(j, h):
+            q, jj = batch_of[j]
+            bank = psum.tile([P, 4, P], F32, name="gc%d%d" % (j, h), tag="gc")
+            for s in range(4):
+                nc.tensor.matmul(bank[:, s, :], lhsT=c_sel[:, h, s, :], rhs=gate_rows[q][:, jj, :], start=True, stop=True)
+            banks["gc", j, h] = bank
+
+        def make_h(j, h):
+            nc.vector.tensor_tensor(out=h_grouped[j][:, h], in0=banks["th", j, h][:],
+                                    in1=banks["gc", j, h][:].rearrange("p s n -> p n s"), op=ALU.mult)
+
+        def quantize_h(j):
+            quantize(h_codes[j][:], h_scales[j][:], h_grouped[j][:].rearrange("p h n t -> p (h n t)"))
+
+        def project_up(j, s):
+            bank = shared_bank("z%d%d" % (j, s), [P, 512], F32)
+            for h in range(2):
+                nc.tensor.matmul_mx(out=bank[:], lhsT=h_codes[j][:, P * h:P * (h + 1)].bitcast(FP8X4),
+                                    lhsT_scale=h_scales[j][:, P * h:P * (h + 1)],
+                                    rhs=u_codes[h, s][:].bitcast(FP8X4), rhs_scale=u_scales[h, s][:],
+                                    start=(h == 0), stop=(h == 1))
+            banks["z", j, s] = bank
+
+        def cross_tile(j):
+            if ("cross", j) not in banks:
+                cross = work.tile([P, D], F32, name="cross%d" % j, tag="cross", bufs=5)
+                banks["cross", j] = cross
+            return banks["cross", j]
+
+        def add_b(j, s):
+            cols = slice(512 * s, 512 * (s + 1))
+            nc.vector.tensor_tensor(out=cross_tile(j)[:, cols], in0=banks["z", j, s][:], in1=b_all[:, cols], op=ALU.add)
+
+        def times_x0(j, s):
+            cols = slice(512 * s, 512 * (s + 1))
+            nc.vector.tensor_tensor(out=cross_tile(j)[:, cols], in0=cross_tile(j)[:, cols], in1=x0_sb[j][:, cols], op=ALU.mult)
+
+        def b_columns():
+            bank = shared_bank("b_col_bank", [P, 4, 2], F32)
+            for k in range(4):
+                nc.tensor.matmul(bank[:, k, :], lhsT=b_row[:, 512 + P * k:512 + P * (k + 1)], rhs=ident16[:, 0:2], start=True, stop=True)
+            nc.scalar.copy(out=b_col[:], in_=bank[:])
+
+        def project_up_turned(j):
+            bank = shared_bank("zt%d" % j, [P, 4, P], F32)
+            for k in range(4):
+                cols = slice(P * k, P * (k + 1))
+                for h in range(2):
+                    nc.tensor.matmul_mx(out=bank[:, k, :], lhsT=u_codes[h, 1][:, cols].bitcast(FP8X4),
+                                        lhsT_scale=u_scales[h, 1][:, cols],
+                                        rhs=h_codes[j][:, P * h:P * (h + 1)].bitcast(FP8X4),
+                                        rhs_scale=h_scales[j][:, P * h:P * (h + 1)], start=(h == 0), stop=(h == 1))
+            zt = work.tile([P, 4, P], F32, name="zt_sb%d" % j, tag="zt_sb", bufs=2)
+            for k in range(4):
+                nc.scalar.activation(out=zt[:, k, :], in_=bank[:, k, :], func=ACT.Identity, bias=b_col[:, k, 0:1])
+            banks["zt", j] = zt
+
+        def turn_back(j):
+            bank = shared_bank("zb%d" % j, [P, 4, P], F32)
+            for k in range(4):
+                nc.tensor.transpose(bank[:, k, :], banks["zt", j][:, k, :], ident32[:])
+            banks["zb", j] = bank
+
+        def times_x0_turned(j):
+            nc.vector.tensor_tensor(out=cross_tile(j)[:, 512:], in0=banks["zb", j][:].rearrange("p k n -> p (k n)"),
+                                    in1=x0_sb[j][:, 512:], op=ALU.mult)
+
+        def add_x(engine, j, lo, hi):
+            if ("res", j) not in banks:
+                res = work.tile([P, D], F32, name="res%d" % j, tag="res", bufs=3)
+                banks["res", j] = res
+            engine.tensor_tensor(out=banks["res", j][:, lo:hi], in0=cross_tile(j)[:, lo:hi], in1=x_sb[j][:, lo:hi], op=ALU.add)
+
+        def store(j, lo, hi):
+            nc.sync.dma_start(out=out[j * P:(j + 1) * P, lo:hi], in_=banks["res", j][:, lo:hi])
+
+        def p_tanh(j, h):
+            project_down(j, h)
+            tanh_p(j, h)
+
+        def x_in(j):
+            turn_x(j)
+            empty_x(j)
+
+        turn_x(0)
+        turn_x(1)
+        widen_v("V", 0, 0)
+        widen_v("S", 0, 1)
+        empty_x(0)
+        empty_x(1)
+        group_v("V", 0, 0)
+        gate_logits(0)
+        gate_logits(1)
+        turn_x(2)
+        turn_x(3)
+        widen_v("V", 1, 0)
+        widen_v("S", 1, 1, range(3))
+        quantize_v(0, 0)
+        sm = softmax_steps(0)
+        sm[0]()
+        empty_x(2)
+        quantize_x(0)
+        sm[1]()
+        sm[2]()
+        empty_x(3)
+        widen_v("S", 1, 1, range(3, 4))
+        turn_x(4)
+        turn_x(5)
+        group_v("V", 1, 0)
+        sm[3]()
+        quantize_x(1)
+        sm[4]()
+        quantize_v(1, 0)
+        sm[5]()
+        select_c()
+        sm[6]()
+        empty_x(4)
+        empty_x(5)
+        gate_logits(2)
+        gate_logits(3)
+        turn_x(6)
+        turn_x(7)
+        empty_x(6)
+        empty_x(7)
+        quantize_x(2)
+        sm[7]()
+        quantize_x(3)
+        sm[8]()
+        group_v("V", 0, 1)
+        sm[9]()
+        p_tanh(0, 0)
+        turn_gate(0)
+        p_tanh(1, 0)
+        gate_logits(4)
+        gate_logits(5)
+        gate_times_c(0, 0)
+        gate_times_c(1, 0)
+        gate_logits(6)
+        gate_logits(7)
+        group_u("S", 0, 0)
+        group_v("V", 1, 1)
+        quantize_v(0, 1)
+        quantize_x(4)
+        quantize_v(1, 1)
+        make_h(0, 0)
+        make_h(1, 0)
+        p_tanh(0, 1)
+        p_tanh(1, 1)
+        gate_times_c(0, 1)
+        gate_times_c(1, 1)
+        sm = softmax_steps(1)
+        sm[0]()
+        quantize_u(0, 0)
+        sm[1]()
+        sm[2]()
+        group_u("S", 1, 0)
+        spread_b()
+        if TURNED:
+            b_columns()
+        group_u("S", 0, 1)
+        group_u(U11, 1, 1)
+        sm[3]()
+        make_h(0, 1)
+        sm[4]()
+        make_h(1, 1)
+        sm[5]()
+        quantize_h(0)
+        sm[6]()
+        quantize_h(1)
+        sm[7]()
+        quantize_u(1, 0)
+        sm[8]()
+        quantize_x(5)
+        sm[9]()
+        project_up(0, 0)
+        p_tanh(2, 0)
+        turn_gate(1)
+        p_tanh(2, 1)
+        quantize_u(1, 1)
+        quantize_x(6)
+        add_b(0, 0)
+        quantize_u(0, 1)
+        quantize_x(7)
+
+        if TURNED:
+            project_up_turned(0)
+        for i in range(1, TILES + 1):
+            make, fetch, done = i + 1, i + 2, i - 1
+            if make < TILES:
+                gate_times_c(make, 0)
+            if i < TILES:
+                project_up(i, 0)
+            if make < TILES:
+                gate_times_c(make, 1)
+            if TURNED:
+                turn_back(done)
+            else:
+                project_up(done, 1)
+            if TURNED and i < TILES:
+                project_up_turned(i)
+            if make < TILES:
+                make_h(make, 0)
+            if i < TILES:
+                add_b(i, 0)
+            if make < TILES:
+                make_h(make, 1)
+            if TURNED:
+                times_x0_turned(done)
+            else:
+                add_b(done, 1)
+            if fetch < TILES:
+                p_tanh(fetch, 0)
+                p_tanh(fetch, 1)
+            if make < TILES:
+                quantize_h(make)
+            if not TURNED:
+                times_x0(done, 0)
+            if done < TILES - 1:
+                times_x0(done, 0 if TURNED else 1)
+            if done < TILES - 2:
+                share = ADD_G if done < TILES - 3 else ADD_G // 2
+                if share < D:
+                    add_x(nc.vector, done, share, D)
+                if share > 0:
+                    add_x(nc.gpsimd, done, 0, share)
+                store(done, 0, D)
+            elif done == TILES - 2:
+                add_x(nc.vector, done, 512, D)
+                store(done, 512, D)
+                if TURNED:
+                    times_x0(done + 1, 0)
+                add_x(nc.vector, done, 0, 512)
+                store(done, 0, 512)
+                if TURNED:
+                    add_x(nc.vector, done + 1, 0, 512)
+                    store(done + 1, 0, 512)
+            else:
+                if not TURNED:
+                    times_x0(done, 1)
+                    add_x(nc.vector, done, 0, 512)
+                    store(done, 0, 512)
+                add_x(nc.vector, done, 512, D)
+                store(done, 512, D)

@@ -17,11 +17,11 @@ ACT = mybir.ActivationFunctionType
 
 P = 128
 TILES = T // P
-GATE_BATCHES = ((0, 1), (2, 3, 4, 5, 6, 7))
+GATE_BATCHES = ((0, 1, 2, 3), (4, 5, 6, 7))
 GATE_COLS = 16
 TURNED = True
-ADD_G = 768
-LAG = 2
+ADD_G = 896
+LAST_G = 256
 U11 = "V"
 
 
@@ -69,40 +69,41 @@ def tile_dcnmixlowrankcrossexperts_kernel(tc, x0, x, v_bytes, v_scale, wg, c, u,
         gate_tmp = [{n: kept("gate_%s%d" % (n, q), [P, len(GATE_BATCHES[q]), w], F32)
                      for n, w in (("max", 1), ("diff", E), ("exp", E), ("sum", 1), ("inv", 1), ("g", E), ("rest", E))}
                     for q in range(batches)]
-        b_col = kept("b_col", [P, 4, 2], F32)
+        b_col = kept("b_col", [P, 8, 2], F32)
         banks = {}
 
         def shared_bank(name, shape, dtype):
             return psum.tile(shape, dtype, name=name, tag="shared", bufs=4)
 
+        nc.gpsimd.memset(warm[:], 0.0)
+        make_identity(nc, ident32[:])
         nc.scalar.dma_start(out=vscale[:], in_=v_scale.rearrange("(g p t) a o -> p g (t a o)", p=P, t=4))
         nc.scalar.dma_start(out=wg_sb[:].rearrange("p g t e -> p g (t e)"), in_=wg.rearrange("(g p t) e -> p g (t e)", p=P, t=4))
-        nc.vector.memset(warm[:], 0.0)
         nc.scalar.activation(out=warm[:, 1:2], in_=warm[:, 0:1], func=ACT.Exp)
-        nc.vector.memset(c_rows[:], 0.0)
-        nc.vector.memset(b_row[:], 0.0)
+        nc.vector.memset(c_rows[:].bitcast(U32), 0)
+        nc.vector.memset(b_row[:].bitcast(U32), 0)
         for q in range(batches):
-            nc.vector.memset(gate_parts[q][:], 0.0)
-        make_identity(nc, ident32[:])
-        make_identity(nc, ident16[:])
+            nc.vector.memset(gate_parts[q][:].bitcast(U32), 0)
+        nc.vector.tensor_copy(out=ident16[:], in_=ident32[:])
 
-        v_rows = v_bytes.rearrange("(g p t) e r -> g p (t e r)", p=P, t=4)
+        v_rows = v_bytes.rearrange("(g p t) e r -> g p t (e r)", p=P, t=4)
         u_rows = u.rearrange("e r d -> (e r) d").rearrange("(h q t i) d -> h t q i d", h=2, t=4, i=4)
 
         def load_x(j):
             nc.sync.dma_start(out=x_sb[j][:], in_=x[j * P:(j + 1) * P, :])
 
-        nc.sync.dma_start(out=v_raw[0][:].rearrange("p t n -> p (t n)"), in_=v_rows[0])
+        nc.sync.dma_start(out=v_raw[0][:, 0:2, :], in_=v_rows[0][:, 0:2, :])
+        nc.sync.dma_start(out=v_raw[0][:, 2:4, :], in_=v_rows[0][:, 2:4, :])
         load_x(0)
         load_x(1)
-        nc.sync.dma_start(out=v_raw[1][:].rearrange("p t n -> p (t n)"), in_=v_rows[1])
-        load_x(2)
-        load_x(3)
+        nc.sync.dma_start(out=v_raw[1][:], in_=v_rows[1])
+        for j in range(2, 4):
+            load_x(j)
         for e in range(E):
             nc.sync.dma_start(out=c_rows[4 * e:4 * e + 4, e * R:(e + 1) * R], in_=c[e].partition_broadcast(4))
-        nc.sync.dma_start(out=b_row[0:1, :], in_=b.rearrange("(o d) -> o d", o=1))
         for j in range(4, TILES):
             load_x(j)
+        nc.sync.dma_start(out=b_row[0:1, :], in_=b.rearrange("(o d) -> o d", o=1))
         for h in range(2):
             for t in range(4):
                 nc.sync.dma_start(out=u_raw[h][:, t, :], in_=u_rows[h][t])
@@ -134,9 +135,9 @@ def tile_dcnmixlowrankcrossexperts_kernel(tc, x0, x, v_bytes, v_scale, wg, c, u,
         def quantize_v(g, h):
             quantize(v_codes[g, h][:], v_scales[g, h][:], v_grouped[g, h][:])
 
-        def group_u(engine, h, s):
-            copy_on(engine, u_grouped[h, s][:].rearrange("p (q i t) -> p q t i", i=4, t=4),
-                    u_raw[h][:, :, 512 * s:512 * (s + 1)].rearrange("p t (q i) -> p q t i", i=4))
+        def group_u(engine, h, s, lo=0, hi=512):
+            copy_on(engine, u_grouped[h, s][:, 4 * lo:4 * hi].rearrange("p (q i t) -> p q t i", i=4, t=4),
+                    u_raw[h][:, :, 512 * s + lo:512 * s + hi].rearrange("p t (q i) -> p q t i", i=4))
 
         def quantize_u(h, s):
             quantize(u_codes[h, s][:], u_scales[h, s][:], u_grouped[h, s][:])
@@ -160,7 +161,7 @@ def tile_dcnmixlowrankcrossexperts_kernel(tc, x0, x, v_bytes, v_scale, wg, c, u,
         def gate_logits(j):
             q, jj = batch_of[j]
             if jj == 0:
-                banks["a", q] = shared_bank("logits%d" % q, [P, len(GATE_BATCHES[q]), E], F32)
+                banks["a", q] = psum.tile([P, len(GATE_BATCHES[q]), E], F32, name="logits%d" % q, tag="gc")
             for g in range(2):
                 for t in range(4):
                     nc.tensor.matmul(banks["a", q][:, jj, :], lhsT=x_grouped[j][:, g, :, t], rhs=wg_sb[:, g, t, :],
@@ -184,10 +185,12 @@ def tile_dcnmixlowrankcrossexperts_kernel(tc, x0, x, v_bytes, v_scale, wg, c, u,
                 lambda: nc.vector.tensor_tensor(out=parts[:, :, :, 2], in0=tmp["rest"][:], in1=parts[:, :, :, 1], op=ALU.subtract),
             ]
 
-        def turn_gate(q):
+        def turn_gate(q, between=None):
             bank = shared_bank("gate_t%d" % q, [P, len(GATE_BATCHES[q]), P], BF16)
             for jj in range(len(GATE_BATCHES[q])):
                 nc.tensor.transpose(bank[:, jj, :], gate_parts[q][:, jj * GATE_COLS:jj * GATE_COLS + P], ident16[:])
+            if between:
+                between()
             nc.scalar.copy(out=gate_rows[q][:], in_=bank[:])
 
         def select_c():
@@ -213,7 +216,7 @@ def tile_dcnmixlowrankcrossexperts_kernel(tc, x0, x, v_bytes, v_scale, wg, c, u,
             banks["p", j, h] = bank
 
         def tanh_p(j, h):
-            th = work.tile([P, P, 4], F32, name="tanh%d%d" % (j, h), tag="tanh", bufs=4)
+            th = work.tile([P, P, 4], F32, name="tanh%d%d" % (j, h), tag="tanh", bufs=6)
             nc.scalar.activation(out=th[:], in_=banks["p", j, h][:].rearrange("p s n -> p n s"), func=ACT.Tanh)
             banks["th", j, h] = th
 
@@ -242,7 +245,7 @@ def tile_dcnmixlowrankcrossexperts_kernel(tc, x0, x, v_bytes, v_scale, wg, c, u,
 
         def cross_tile(j):
             if ("cross", j) not in banks:
-                cross = work.tile([P, D], F32, name="cross%d" % j, tag="cross", bufs=5)
+                cross = work.tile([P, D], F32, name="cross%d" % j, tag="cross", bufs=4)
                 banks["cross", j] = cross
             return banks["cross", j]
 
@@ -255,34 +258,37 @@ def tile_dcnmixlowrankcrossexperts_kernel(tc, x0, x, v_bytes, v_scale, wg, c, u,
             nc.vector.tensor_tensor(out=cross_tile(j)[:, cols], in0=cross_tile(j)[:, cols], in1=x0_sb[j][:, cols], op=ALU.mult)
 
         def b_columns():
-            bank = shared_bank("b_col_bank", [P, 4, 2], F32)
-            for k in range(4):
-                nc.tensor.matmul(bank[:, k, :], lhsT=b_row[:, 512 + P * k:512 + P * (k + 1)], rhs=ident16[:, 0:2], start=True, stop=True)
+            bank = shared_bank("b_col_bank", [P, 8, 2], F32)
+            for k in range(8):
+                nc.tensor.matmul(bank[:, k, :], lhsT=b_row[:, P * k:P * (k + 1)], rhs=ident16[:, 0:2], start=True, stop=True)
             nc.scalar.copy(out=b_col[:], in_=bank[:])
 
-        def project_up_turned(j):
-            bank = shared_bank("zt%d" % j, [P, 4, P], F32)
+        def project_up_turned(j, s):
+            bank = shared_bank("zt%d%d" % (j, s), [P, 4, P], F32)
             for k in range(4):
                 cols = slice(P * k, P * (k + 1))
                 for h in range(2):
-                    nc.tensor.matmul_mx(out=bank[:, k, :], lhsT=u_codes[h, 1][:, cols].bitcast(FP8X4),
-                                        lhsT_scale=u_scales[h, 1][:, cols],
+                    nc.tensor.matmul_mx(out=bank[:, k, :], lhsT=u_codes[h, s][:, cols].bitcast(FP8X4),
+                                        lhsT_scale=u_scales[h, s][:, cols],
                                         rhs=h_codes[j][:, P * h:P * (h + 1)].bitcast(FP8X4),
                                         rhs_scale=h_scales[j][:, P * h:P * (h + 1)], start=(h == 0), stop=(h == 1))
-            zt = work.tile([P, 4, P], F32, name="zt_sb%d" % j, tag="zt_sb", bufs=2)
+            zt = work.tile([P, 4, P], F32, name="zt_sb%d%d" % (j, s), tag="zt_sb", bufs=3)
             for k in range(4):
-                nc.scalar.activation(out=zt[:, k, :], in_=bank[:, k, :], func=ACT.Identity, bias=b_col[:, k, 0:1])
-            banks["zt", j] = zt
+                nc.scalar.activation(out=zt[:, k, :], in_=bank[:, k, :], func=ACT.Identity, bias=b_col[:, 4 * s + k, 0:1])
+            banks["zt", j, s] = zt
 
-        def turn_back(j):
-            bank = shared_bank("zb%d" % j, [P, 4, P], F32)
+        def turn_back(j, s, after=None):
+            bank = shared_bank("zb%d%d" % (j, s), [P, 4, P], F32)
             for k in range(4):
-                nc.tensor.transpose(bank[:, k, :], banks["zt", j][:, k, :], ident32[:])
-            banks["zb", j] = bank
+                nc.tensor.transpose(bank[:, k, :], banks["zt", j, s][:, k, :], ident32[:])
+            banks["zb", j, s] = bank
+            if after:
+                after()
 
-        def times_x0_turned(j):
-            nc.vector.tensor_tensor(out=cross_tile(j)[:, 512:], in0=banks["zb", j][:].rearrange("p k n -> p (k n)"),
-                                    in1=x0_sb[j][:, 512:], op=ALU.mult)
+        def times_x0_turned(j, s):
+            cols = slice(512 * s, 512 * (s + 1))
+            nc.vector.tensor_tensor(out=cross_tile(j)[:, cols], in0=banks["zb", j, s][:].rearrange("p k n -> p (k n)"),
+                                    in1=x0_sb[j][:, cols], op=ALU.mult)
 
         def add_x(engine, j, lo, hi):
             if ("res", j) not in banks:
@@ -309,154 +315,145 @@ def tile_dcnmixlowrankcrossexperts_kernel(tc, x0, x, v_bytes, v_scale, wg, c, u,
         empty_x(1)
         group_v("V", 0, 0)
         gate_logits(0)
-        gate_logits(1)
         turn_x(2)
         turn_x(3)
+        gate_logits(1)
         widen_v("V", 1, 0)
-        widen_v("S", 1, 1, range(3))
-        quantize_v(0, 0)
-        sm = softmax_steps(0)
-        sm[0]()
+        widen_v("S", 1, 1, range(2))
         empty_x(2)
-        quantize_x(0)
-        sm[1]()
-        sm[2]()
         empty_x(3)
-        widen_v("S", 1, 1, range(3, 4))
+        widen_v("S", 1, 1, range(2, 4))
         turn_x(4)
-        turn_x(5)
-        group_v("V", 1, 0)
-        sm[3]()
-        quantize_x(1)
-        sm[4]()
-        quantize_v(1, 0)
-        sm[5]()
-        select_c()
-        sm[6]()
-        empty_x(4)
-        empty_x(5)
         gate_logits(2)
         gate_logits(3)
+        turn_x(5)
+        empty_x(4)
+        empty_x(5)
         turn_x(6)
         turn_x(7)
+        group_v("V", 0, 1)
+        quantize_v(0, 0)
+        group_v("V", 1, 0)
+        quantize_x(0)
+        quantize_v(1, 0)
+        sm = softmax_steps(0)
+        sm[0]()
+        quantize_v(0, 1)
+        sm[1]()
         empty_x(6)
+        sm[2]()
         empty_x(7)
+        group_v("V", 1, 1)
+        sm[3]()
+        gate_logits(4)
+        project_down(0, 0)
+        gate_logits(5)
+        group_u("S", 0, 0, 0, 256)
+        tanh_p(0, 0)
+        quantize_x(1)
+        sm[4]()
+        quantize_v(1, 1)
+        sm[5]()
         quantize_x(2)
+        sm[6]()
+        select_c()
         sm[7]()
         quantize_x(3)
         sm[8]()
-        group_v("V", 0, 1)
+        quantize_x(4)
         sm[9]()
-        p_tanh(0, 0)
-        turn_gate(0)
-        p_tanh(1, 0)
-        gate_logits(4)
-        gate_logits(5)
-        gate_times_c(0, 0)
-        gate_times_c(1, 0)
         gate_logits(6)
         gate_logits(7)
-        group_u("S", 0, 0)
-        group_v("V", 1, 1)
-        quantize_v(0, 1)
-        quantize_x(4)
-        quantize_v(1, 1)
-        make_h(0, 0)
-        make_h(1, 0)
-        p_tanh(0, 1)
-        p_tanh(1, 1)
-        gate_times_c(0, 1)
-        gate_times_c(1, 1)
+        group_u("S", 0, 0, 256, 512)
+        group_u("S", 1, 0, 0, 256)
+        turn_gate(0)
+        project_down(0, 1)
+        tanh_p(0, 1)
+        gate_times_c(0, 0)
+        spread_b()
+        b_columns()
+        project_down(1, 0)
         sm = softmax_steps(1)
+        quantize_x(5)
         sm[0]()
-        quantize_u(0, 0)
+        group_u(U11, 1, 1)
         sm[1]()
         sm[2]()
-        group_u("S", 1, 0)
-        spread_b()
-        if TURNED:
-            b_columns()
+        gate_times_c(0, 1)
+        project_down(1, 1)
+        group_u("S", 1, 0, 256, 512)
+        tanh_p(1, 0)
         group_u("S", 0, 1)
-        group_u(U11, 1, 1)
+        tanh_p(1, 1)
+        quantize_u(0, 0)
+        make_h(0, 0)
+        gate_times_c(1, 0)
+        quantize_u(1, 1)
         sm[3]()
         make_h(0, 1)
+        gate_times_c(1, 1)
         sm[4]()
-        make_h(1, 1)
+        quantize_u(1, 0)
         sm[5]()
         quantize_h(0)
         sm[6]()
-        quantize_h(1)
-        sm[7]()
-        quantize_u(1, 0)
-        sm[8]()
-        quantize_x(5)
-        sm[9]()
+        project_down(2, 0)
         project_up(0, 0)
-        p_tanh(2, 0)
-        turn_gate(1)
-        p_tanh(2, 1)
-        quantize_u(1, 1)
-        quantize_x(6)
+        project_down(2, 1)
+        tanh_p(2, 0)
+        make_h(1, 0)
+        sm[7]()
         add_b(0, 0)
+        sm[8]()
         quantize_u(0, 1)
+        sm[9]()
+        make_h(1, 1)
+        project_up_turned(0, 1)
+        turn_gate(1)
+        tanh_p(2, 1)
+        quantize_x(6)
+        quantize_h(1)
         quantize_x(7)
 
-        if TURNED:
-            project_up_turned(0)
-        for i in range(1, TILES + 1):
+        for i in range(1, TILES):
             make, fetch, done = i + 1, i + 2, i - 1
-            if make < TILES:
+            last = i == TILES - 1
+            if last:
+                turn_back(done, 1)
+                project_up_turned(i, 0)
+            else:
                 gate_times_c(make, 0)
-            if i < TILES:
-                project_up(i, 0)
-            if make < TILES:
+                turn_back(done, 1)
                 gate_times_c(make, 1)
-            if TURNED:
-                turn_back(done)
-            else:
-                project_up(done, 1)
-            if TURNED and i < TILES:
-                project_up_turned(i)
-            if make < TILES:
+                project_up(i, 0)
+            project_up_turned(i, 1)
+            if not last:
                 make_h(make, 0)
-            if i < TILES:
-                add_b(i, 0)
-            if make < TILES:
+            times_x0_turned(done, 1)
+            if not last:
                 make_h(make, 1)
-            if TURNED:
-                times_x0_turned(done)
-            else:
-                add_b(done, 1)
+                add_b(i, 0)
             if fetch < TILES:
                 p_tanh(fetch, 0)
                 p_tanh(fetch, 1)
-            if make < TILES:
+            if done >= 1 and ADD_G < D:
+                add_x(nc.vector, done - 1, ADD_G if done - 1 < TILES - 3 else LAST_G, D)
+                store(done - 1, 0, D)
+            times_x0(done, 0)
+            if not last:
                 quantize_h(make)
-            if not TURNED:
-                times_x0(done, 0)
-            if done < TILES - 1:
-                times_x0(done, 0 if TURNED else 1)
-            if done < TILES - 2:
-                share = ADD_G if done < TILES - 3 else ADD_G // 2
-                if share < D:
-                    add_x(nc.vector, done, share, D)
-                if share > 0:
-                    add_x(nc.gpsimd, done, 0, share)
-                store(done, 0, D)
-            elif done == TILES - 2:
-                add_x(nc.vector, done, 512, D)
-                store(done, 512, D)
-                if TURNED:
-                    times_x0(done + 1, 0)
-                add_x(nc.vector, done, 0, 512)
-                store(done, 0, 512)
-                if TURNED:
-                    add_x(nc.vector, done + 1, 0, 512)
-                    store(done + 1, 0, 512)
-            else:
-                if not TURNED:
-                    times_x0(done, 1)
-                    add_x(nc.vector, done, 0, 512)
-                    store(done, 0, 512)
-                add_x(nc.vector, done, 512, D)
-                store(done, 512, D)
+                add_x(nc.gpsimd, done, 0, ADD_G if done < TILES - 3 else LAST_G)
+                if ADD_G == D:
+                    store(done, 0, D)
+        done, last = TILES - 2, TILES - 1
+        add_x(nc.vector, done, 512, D)
+        store(done, 512, D)
+        turn_back(last, 0)
+        turn_back(last, 1)
+        add_x(nc.vector, done, 0, 512)
+        store(done, 0, 512)
+        times_x0_turned(last, 0)
+        times_x0_turned(last, 1)
+        for s in range(2):
+            add_x(nc.vector, last, 512 * s, 512 * (s + 1))
+            store(last, 512 * s, 512 * (s + 1))

@@ -21,7 +21,7 @@ GATE_BATCHES = ((0, 1, 2, 3), (4, 5, 6, 7))
 GATE_COLS = 16
 TURNED = True
 ADD_G = 896
-LAST_G = 256
+LAST_G = 896
 U11 = "V"
 
 
@@ -42,7 +42,6 @@ def tile_dcnmixlowrankcrossexperts_kernel(tc, x0, x, v_bytes, v_scale, wg, c, u,
         wg_sb = kept("wg_sb", [P, 2, 4, E], BF16)
         c_rows = kept("c_rows", [P, E * R], BF16)
         c_sel = kept("c_sel", [P, 2, 4, P], BF16)
-        b_row = kept("b_row", [P, D], BF16)
         b_all = kept("b_all", [P, D], BF16)
         warm = kept("warm", [P, 2], F32)
         v_raw = [kept("v_raw%d" % g, [P, 4, E * R], U8) for g in range(2)]
@@ -54,12 +53,14 @@ def tile_dcnmixlowrankcrossexperts_kernel(tc, x0, x, v_bytes, v_scale, wg, c, u,
         u_grouped = {(h, s): kept("u_grouped%d%d" % (h, s), [P, 2048], BF16) for h in range(2) for s in range(2)}
         u_codes = {(h, s): kept("u_codes%d%d" % (h, s), [P, 512], U32) for h in range(2) for s in range(2)}
         u_scales = {(h, s): kept("u_scales%d%d" % (h, s), [P, 512], U8) for h in range(2) for s in range(2)}
-        x_sb = [kept("x_sb%d" % j, [P, D], BF16) for j in range(TILES)]
+        x_all = kept("x_all", [P, TILES * D], BF16)
+        x_sb = [x_all[:, j * D:(j + 1) * D] for j in range(TILES)]
+        cross = kept("cross", [P, TILES * D], F32)
         x0_sb = [kept("x0_sb%d" % j, [P, D], BF16) for j in range(TILES)]
         x_grouped = [kept("x_grouped%d" % j, [P, 2, P, 4], BF16) for j in range(TILES)]
         x_codes = [kept("x_codes%d" % j, [P, 2 * P], U32) for j in range(TILES)]
         x_scales = [kept("x_scales%d" % j, [P, 2 * P], U8) for j in range(TILES)]
-        h_grouped = [kept("h_grouped%d" % j, [P, 2, P, 4], BF16) for j in range(TILES)]
+        h_grouped = {}
         h_codes = [kept("h_codes%d" % j, [P, 2 * P], U32) for j in range(TILES)]
         h_scales = [kept("h_scales%d" % j, [P, 2 * P], U8) for j in range(TILES)]
         batches = len(GATE_BATCHES)
@@ -81,7 +82,6 @@ def tile_dcnmixlowrankcrossexperts_kernel(tc, x0, x, v_bytes, v_scale, wg, c, u,
         nc.scalar.dma_start(out=wg_sb[:].rearrange("p g t e -> p g (t e)"), in_=wg.rearrange("(g p t) e -> p g (t e)", p=P, t=4))
         nc.scalar.activation(out=warm[:, 1:2], in_=warm[:, 0:1], func=ACT.Exp)
         nc.vector.memset(c_rows[:].bitcast(U32), 0)
-        nc.vector.memset(b_row[:].bitcast(U32), 0)
         for q in range(batches):
             nc.vector.memset(gate_parts[q][:].bitcast(U32), 0)
         nc.vector.tensor_copy(out=ident16[:], in_=ident32[:])
@@ -90,7 +90,7 @@ def tile_dcnmixlowrankcrossexperts_kernel(tc, x0, x, v_bytes, v_scale, wg, c, u,
         u_rows = u.rearrange("e r d -> (e r) d").rearrange("(h q t i) d -> h t q i d", h=2, t=4, i=4)
 
         def load_x(j):
-            nc.sync.dma_start(out=x_sb[j][:], in_=x[j * P:(j + 1) * P, :])
+            nc.sync.dma_start(out=x_sb[j], in_=x[j * P:(j + 1) * P, :])
 
         nc.sync.dma_start(out=v_raw[0][:, 0:2, :], in_=v_rows[0][:, 0:2, :])
         nc.sync.dma_start(out=v_raw[0][:, 2:4, :], in_=v_rows[0][:, 2:4, :])
@@ -103,10 +103,10 @@ def tile_dcnmixlowrankcrossexperts_kernel(tc, x0, x, v_bytes, v_scale, wg, c, u,
             nc.sync.dma_start(out=c_rows[4 * e:4 * e + 4, e * R:(e + 1) * R], in_=c[e].partition_broadcast(4))
         for j in range(4, TILES):
             load_x(j)
-        nc.sync.dma_start(out=b_row[0:1, :], in_=b.rearrange("(o d) -> o d", o=1))
         for h in range(2):
             for t in range(4):
                 nc.sync.dma_start(out=u_raw[h][:, t, :], in_=u_rows[h][t])
+        nc.sync.dma_start(out=b_all[:], in_=b.partition_broadcast(P))
         for j in range(TILES):
             nc.sync.dma_start(out=x0_sb[j][:], in_=x0[j * P:(j + 1) * P, :])
 
@@ -144,7 +144,7 @@ def tile_dcnmixlowrankcrossexperts_kernel(tc, x0, x, v_bytes, v_scale, wg, c, u,
 
         def turn_x(j):
             bank = shared_bank("xt%d" % j, [P, 4, P], F32)
-            words = x_sb[j][:].bitcast(F32)
+            words = x_sb[j].bitcast(F32)
             for g in range(2):
                 for w in range(2):
                     nc.tensor.transpose(bank[:, 2 * g + w, :], words[:, 256 * g + w:256 * (g + 1):2], ident32[:])
@@ -197,13 +197,6 @@ def tile_dcnmixlowrankcrossexperts_kernel(tc, x0, x, v_bytes, v_scale, wg, c, u,
             nc.vector.tensor_copy(out=c_sel[:].rearrange("p h s (q i) -> p h s q i", i=4),
                                   in_=c_rows[:].rearrange("p (h q s i) -> p h s q i", h=2, s=4, i=4))
 
-        def spread_b():
-            bank = shared_bank("b_bank", [P, D], BF16)
-            for s in range(2):
-                nc.tensor.matmul(bank[:, 512 * s:512 * (s + 1)], lhsT=ident16[:, 0:1].to_broadcast([P, P]),
-                                 rhs=b_row[:, 512 * s:512 * (s + 1)], start=True, stop=True)
-            nc.scalar.copy(out=b_all[:], in_=bank[:])
-
         def project_down(j, h):
             bank = psum.tile([P, 4, P], F32, name="p%d%d" % (j, h), tag="p")
             for s in range(4):
@@ -228,6 +221,8 @@ def tile_dcnmixlowrankcrossexperts_kernel(tc, x0, x, v_bytes, v_scale, wg, c, u,
             banks["gc", j, h] = bank
 
         def make_h(j, h):
+            if j not in h_grouped:
+                h_grouped[j] = work.tile([P, 2, P, 4], BF16, name="h_grouped%d" % j, tag="h_grouped", bufs=3, align_bytes=64)
             nc.vector.tensor_tensor(out=h_grouped[j][:, h], in0=banks["th", j, h][:],
                                     in1=banks["gc", j, h][:].rearrange("p s n -> p n s"), op=ALU.mult)
 
@@ -244,10 +239,7 @@ def tile_dcnmixlowrankcrossexperts_kernel(tc, x0, x, v_bytes, v_scale, wg, c, u,
             banks["z", j, s] = bank
 
         def cross_tile(j):
-            if ("cross", j) not in banks:
-                cross = work.tile([P, D], F32, name="cross%d" % j, tag="cross", bufs=4)
-                banks["cross", j] = cross
-            return banks["cross", j]
+            return cross[:, j * D:(j + 1) * D]
 
         def add_b(j, s):
             cols = slice(512 * s, 512 * (s + 1))
@@ -257,11 +249,14 @@ def tile_dcnmixlowrankcrossexperts_kernel(tc, x0, x, v_bytes, v_scale, wg, c, u,
             cols = slice(512 * s, 512 * (s + 1))
             nc.vector.tensor_tensor(out=cross_tile(j)[:, cols], in0=cross_tile(j)[:, cols], in1=x0_sb[j][:, cols], op=ALU.mult)
 
-        def b_columns():
+        def b_columns_mm():
             bank = shared_bank("b_col_bank", [P, 8, 2], F32)
             for k in range(8):
-                nc.tensor.matmul(bank[:, k, :], lhsT=b_row[:, P * k:P * (k + 1)], rhs=ident16[:, 0:2], start=True, stop=True)
-            nc.scalar.copy(out=b_col[:], in_=bank[:])
+                nc.tensor.matmul(bank[:, k, :], lhsT=b_all[:, P * k:P * (k + 1)], rhs=ident16[:, 0:2], start=True, stop=True)
+            banks["b_col"] = bank
+
+        def b_columns_copy():
+            nc.scalar.copy(out=b_col[:], in_=banks["b_col"][:])
 
         def project_up_turned(j, s):
             bank = shared_bank("zt%d%d" % (j, s), [P, 4, P], F32)
@@ -290,14 +285,12 @@ def tile_dcnmixlowrankcrossexperts_kernel(tc, x0, x, v_bytes, v_scale, wg, c, u,
             nc.vector.tensor_tensor(out=cross_tile(j)[:, cols], in0=banks["zb", j, s][:].rearrange("p k n -> p (k n)"),
                                     in1=x0_sb[j][:, cols], op=ALU.mult)
 
-        def add_x(engine, j, lo, hi):
-            if ("res", j) not in banks:
-                res = work.tile([P, D], F32, name="res%d" % j, tag="res", bufs=3)
-                banks["res", j] = res
-            engine.tensor_tensor(out=banks["res", j][:, lo:hi], in0=cross_tile(j)[:, lo:hi], in1=x_sb[j][:, lo:hi], op=ALU.add)
+        def add_x(engine, lo, hi):
+            engine.tensor_tensor(out=cross[:, lo:hi], in0=cross[:, lo:hi], in1=x_all[:, lo:hi], op=ALU.add)
 
-        def store(j, lo, hi):
-            nc.sync.dma_start(out=out[j * P:(j + 1) * P, lo:hi], in_=banks["res", j][:, lo:hi])
+        def store(lo, hi):
+            j = lo // D
+            nc.sync.dma_start(out=out[j * P:(j + 1) * P, lo - j * D:hi - j * D], in_=cross[:, lo:hi])
 
         def p_tanh(j, h):
             project_down(j, h)
@@ -314,6 +307,7 @@ def tile_dcnmixlowrankcrossexperts_kernel(tc, x0, x, v_bytes, v_scale, wg, c, u,
         empty_x(0)
         empty_x(1)
         group_v("V", 0, 0)
+        group_v("V", 0, 1)
         gate_logits(0)
         turn_x(2)
         turn_x(3)
@@ -331,7 +325,6 @@ def tile_dcnmixlowrankcrossexperts_kernel(tc, x0, x, v_bytes, v_scale, wg, c, u,
         empty_x(5)
         turn_x(6)
         turn_x(7)
-        group_v("V", 0, 1)
         quantize_v(0, 0)
         group_v("V", 1, 0)
         quantize_x(0)
@@ -354,9 +347,9 @@ def tile_dcnmixlowrankcrossexperts_kernel(tc, x0, x, v_bytes, v_scale, wg, c, u,
         sm[4]()
         quantize_v(1, 1)
         sm[5]()
-        quantize_x(2)
-        sm[6]()
         select_c()
+        sm[6]()
+        quantize_x(2)
         sm[7]()
         quantize_x(3)
         sm[8]()
@@ -368,32 +361,32 @@ def tile_dcnmixlowrankcrossexperts_kernel(tc, x0, x, v_bytes, v_scale, wg, c, u,
         group_u("S", 1, 0, 0, 256)
         turn_gate(0)
         project_down(0, 1)
-        tanh_p(0, 1)
         gate_times_c(0, 0)
-        spread_b()
-        b_columns()
         project_down(1, 0)
+        group_u("S", 1, 0, 256, 512)
+        tanh_p(0, 1)
         sm = softmax_steps(1)
         quantize_x(5)
-        sm[0]()
         group_u(U11, 1, 1)
+        sm[0]()
+        quantize_u(0, 0)
         sm[1]()
         sm[2]()
         gate_times_c(0, 1)
-        project_down(1, 1)
-        group_u("S", 1, 0, 256, 512)
         tanh_p(1, 0)
-        group_u("S", 0, 1)
+        project_down(1, 1)
+        group_u("S", 0, 1, 0, 256)
         tanh_p(1, 1)
-        quantize_u(0, 0)
+        group_u("S", 0, 1, 256, 512)
+        quantize_u(1, 1)
         make_h(0, 0)
         gate_times_c(1, 0)
-        quantize_u(1, 1)
+        quantize_u(1, 0)
         sm[3]()
         make_h(0, 1)
         gate_times_c(1, 1)
         sm[4]()
-        quantize_u(1, 0)
+        quantize_x(6)
         sm[5]()
         quantize_h(0)
         sm[6]()
@@ -401,59 +394,84 @@ def tile_dcnmixlowrankcrossexperts_kernel(tc, x0, x, v_bytes, v_scale, wg, c, u,
         project_up(0, 0)
         project_down(2, 1)
         tanh_p(2, 0)
+        tanh_p(2, 1)
         make_h(1, 0)
         sm[7]()
-        add_b(0, 0)
-        sm[8]()
-        quantize_u(0, 1)
-        sm[9]()
-        make_h(1, 1)
-        project_up_turned(0, 1)
-        turn_gate(1)
-        tanh_p(2, 1)
-        quantize_x(6)
-        quantize_h(1)
         quantize_x(7)
+        sm[8]()
+        make_h(1, 1)
+        sm[9]()
+        add_b(0, 0)
+        b_columns_mm()
+        turn_gate(1)
+        b_columns_copy()
+        quantize_u(0, 1)
+        quantize_h(1)
+        times_x0(0, 0)
 
-        for i in range(1, TILES):
+        add_x(nc.gpsimd, 0, 512)
+        store(0, 512)
+        for i in range(1, TILES - 1):
             make, fetch, done = i + 1, i + 2, i - 1
-            last = i == TILES - 1
-            if last:
+            plain = i < TILES - 2
+            gate_times_c(make, 0)
+            if i == 1:
+                gate_times_c(make, 1)
+                p_tanh(fetch, 0)
+                project_up_turned(done, 1)
+                project_up(i, 0)
                 turn_back(done, 1)
-                project_up_turned(i, 0)
             else:
-                gate_times_c(make, 0)
                 turn_back(done, 1)
                 gate_times_c(make, 1)
-                project_up(i, 0)
+                if plain:
+                    project_up(i, 0)
+                else:
+                    project_up_turned(i, 0)
             project_up_turned(i, 1)
-            if not last:
-                make_h(make, 0)
-            times_x0_turned(done, 1)
-            if not last:
+            make_h(make, 0)
+            if i == 1:
                 make_h(make, 1)
                 add_b(i, 0)
+                times_x0_turned(done, 1)
+            else:
+                times_x0_turned(done, 1)
+                if plain:
+                    add_b(i, 0)
+                make_h(make, 1)
             if fetch < TILES:
-                p_tanh(fetch, 0)
+                if i > 1:
+                    p_tanh(fetch, 0)
                 p_tanh(fetch, 1)
-            if done >= 1 and ADD_G < D:
-                add_x(nc.vector, done - 1, ADD_G if done - 1 < TILES - 3 else LAST_G, D)
-                store(done - 1, 0, D)
-            times_x0(done, 0)
-            if not last:
-                quantize_h(make)
-                add_x(nc.gpsimd, done, 0, ADD_G if done < TILES - 3 else LAST_G)
-                if ADD_G == D:
-                    store(done, 0, D)
+            if i >= 2 and plain:
+                lo = done * D - 512
+                add_x(nc.vector, lo + ADD_G, lo + D)
+                store(lo + 512, lo + D)
+            if plain:
+                times_x0(i, 0)
+            quantize_h(make)
+            lo = i * D - 512
+            share = ADD_G if i < TILES - 3 else (LAST_G if plain else 512)
+            add_x(nc.gpsimd, lo, lo + share)
+            store(lo, lo + 512)
         done, last = TILES - 2, TILES - 1
-        add_x(nc.vector, done, 512, D)
-        store(done, 512, D)
+        turn_back(done, 0)
+        turn_back(done, 1)
+        project_up_turned(last, 0)
+        project_up_turned(last, 1)
+        times_x0_turned(done, 0)
+        times_x0_turned(done, 1)
+        lo = (done - 1) * D - 512
+        add_x(nc.vector, lo + LAST_G, lo + D)
+        store(lo + 512, lo + D)
+        add_x(nc.vector, done * D, done * D + 512)
+        store(done * D, done * D + 512)
         turn_back(last, 0)
         turn_back(last, 1)
-        add_x(nc.vector, done, 0, 512)
-        store(done, 0, 512)
+        add_x(nc.vector, done * D + 512, last * D)
+        store(done * D + 512, last * D)
         times_x0_turned(last, 0)
         times_x0_turned(last, 1)
-        for s in range(2):
-            add_x(nc.vector, last, 512 * s, 512 * (s + 1))
-            store(last, 512 * s, 512 * (s + 1))
+        for lo, hi in ((0, 512), (512, D)):
+            add_x(nc.vector, last * D + lo, last * D + hi)
+            store(last * D + lo, last * D + hi)

@@ -14,15 +14,16 @@ FP8 = mybir.dt.float8_e4m3fn
 FP8X4 = mybir.dt.float8_e4m3fn_x4
 ALU = mybir.AluOpType
 ACT = mybir.ActivationFunctionType
+AXIS_X = mybir.AxisListType.X
 
 P = 128
+PACK = 4
+HALF = 512
 TILES = T // P
-GATE_BATCHES = ((0, 1, 2, 3), (4, 5, 6, 7))
-GATE_COLS = 16
-TURNED = True
-ADD_G = 896
-LAST_G = 896
-U11 = "V"
+GATE_TILES = 4
+GATE_ROWS = 16
+BOTH = (0, 1)
+QUARTERS = ((0, 0), (0, 1), (1, 0), (1, 1))
 
 
 def tile_dcnmixlowrankcrossexperts_kernel(tc, x0, x, v_bytes, v_scale, wg, c, u, b, out):
@@ -36,287 +37,303 @@ def tile_dcnmixlowrankcrossexperts_kernel(tc, x0, x, v_bytes, v_scale, wg, c, u,
         def kept(name, shape, dtype):
             return keep.tile(shape, dtype, name=name, align_bytes=64)
 
-        ident32 = kept("ident32", [P, P], F32)
-        ident16 = kept("ident16", [P, P], BF16)
-        vscale = kept("vscale", [P, 2, 4], F32)
-        wg_sb = kept("wg_sb", [P, 2, 4, E], BF16)
-        c_rows = kept("c_rows", [P, E * R], BF16)
-        c_sel = kept("c_sel", [P, 2, 4, P], BF16)
-        b_all = kept("b_all", [P, D], BF16)
-        warm = kept("warm", [P, 2], F32)
-        v_raw = [kept("v_raw%d" % g, [P, 4, E * R], U8) for g in range(2)]
-        v_wide = {(g, h): kept("v_wide%d%d" % (g, h), [P, 4, 512], BF16) for g in range(2) for h in range(2)}
-        v_grouped = {(g, h): kept("v_grouped%d%d" % (g, h), [P, 2048], BF16) for g in range(2) for h in range(2)}
-        v_codes = {(g, h): kept("v_codes%d%d" % (g, h), [P, 512], U32) for g in range(2) for h in range(2)}
-        v_scales = {(g, h): kept("v_scales%d%d" % (g, h), [P, 512], U8) for g in range(2) for h in range(2)}
-        u_raw = [kept("u_raw%d" % h, [P, 4, D], BF16) for h in range(2)]
-        u_grouped = {(h, s): kept("u_grouped%d%d" % (h, s), [P, 2048], BF16) for h in range(2) for s in range(2)}
-        u_codes = {(h, s): kept("u_codes%d%d" % (h, s), [P, 512], U32) for h in range(2) for s in range(2)}
-        u_scales = {(h, s): kept("u_scales%d%d" % (h, s), [P, 512], U8) for h in range(2) for s in range(2)}
-        x_all = kept("x_all", [P, TILES * D], BF16)
-        x_sb = [x_all[:, j * D:(j + 1) * D] for j in range(TILES)]
-        cross = kept("cross", [P, TILES * D], F32)
-        x0_sb = [kept("x0_sb%d" % j, [P, D], BF16) for j in range(TILES)]
-        x_grouped = [kept("x_grouped%d" % j, [P, 2, P, 4], BF16) for j in range(TILES)]
-        x_codes = [kept("x_codes%d" % j, [P, 2 * P], U32) for j in range(TILES)]
-        x_scales = [kept("x_scales%d" % j, [P, 2 * P], U8) for j in range(TILES)]
-        h_grouped = {}
-        h_codes = [kept("h_codes%d" % j, [P, 2 * P], U32) for j in range(TILES)]
-        h_scales = [kept("h_scales%d" % j, [P, 2 * P], U8) for j in range(TILES)]
-        batches = len(GATE_BATCHES)
-        batch_of = {j: (q, jj) for q in range(batches) for jj, j in enumerate(GATE_BATCHES[q])}
-        gate_parts = [kept("gate_parts%d" % q, [P, (len(GATE_BATCHES[q]) - 1) * GATE_COLS + P], BF16) for q in range(batches)]
-        gate_rows = [kept("gate_rows%d" % q, [P, len(GATE_BATCHES[q]), P], BF16) for q in range(batches)]
-        gate_tmp = [{n: kept("gate_%s%d" % (n, q), [P, len(GATE_BATCHES[q]), w], F32)
-                     for n, w in (("max", 1), ("diff", E), ("exp", E), ("sum", 1), ("inv", 1), ("g", E), ("rest", E))}
-                    for q in range(batches)]
-        b_col = kept("b_col", [P, 8, 2], F32)
-        banks = {}
+        def quarters(name, shape, dtype):
+            return {key: kept("%s%d%d" % (name, key[0], key[1]), shape, dtype) for key in QUARTERS}
 
         def shared_bank(name, shape, dtype):
             return psum.tile(shape, dtype, name=name, tag="shared", bufs=4)
 
-        nc.gpsimd.memset(warm[:], 0.0)
+        ident32 = kept("ident32", [P, P], F32)
+        ident16 = kept("ident16", [P, P], BF16)
+        table_warmup = kept("table_warmup", [P, 2], F32)
+        vscale = kept("vscale", [P, 2, PACK], F32)
+        wg_sb = kept("wg_sb", [P, 2, PACK, E], BF16)
+        c_rows = kept("c_rows", [P, E * R], BF16)
+        c_sel = kept("c_sel", [P, 2, PACK, P], BF16)
+        b_all = kept("b_all", [P, D], BF16)
+        b_col = kept("b_col", [P, D // P, 2], F32)
+        v_raw = [kept("v_raw%d" % dp, [P, PACK, E * R], U8) for dp in BOTH]
+        v_wide = quarters("v_wide", [P, PACK, HALF], BF16)
+        v_grouped = quarters("v_grouped", [P, PACK * HALF], BF16)
+        v_codes = quarters("v_codes", [P, HALF], U32)
+        v_scales = quarters("v_scales", [P, HALF], U8)
+        u_raw = [kept("u_raw%d" % rp, [P, PACK, D], BF16) for rp in BOTH]
+        u_grouped = quarters("u_grouped", [P, PACK * HALF], BF16)
+        u_codes = quarters("u_codes", [P, HALF], U32)
+        u_scales = quarters("u_scales", [P, HALF], U8)
+        x_all = kept("x_all", [P, TILES * D], BF16)
+        cross = kept("cross", [P, TILES * D], F32)
+        x0_sb = [kept("x0_sb%d" % j, [P, D], BF16) for j in range(TILES)]
+        x_grouped = [kept("x_grouped%d" % m, [P, 2, 2, P, PACK], BF16) for m in range(TILES // 2)]
+        x_codes = [kept("x_codes%d" % m, [P, 2, 2, P], U32) for m in range(TILES // 2)]
+        x_scales = [kept("x_scales%d" % m, [P, 2, 2, P], U8) for m in range(TILES // 2)]
+        h_codes = [kept("h_codes%d" % j, [P, 2, P], U32) for j in range(TILES)]
+        h_scales = [kept("h_scales%d" % j, [P, 2, P], U8) for j in range(TILES)]
+        gate_parts = [kept("gate_parts%d" % q, [P, (GATE_TILES - 1) * GATE_ROWS + P], BF16) for q in BOTH]
+        gate_rows = [kept("gate_rows%d" % q, [P, GATE_TILES, P], BF16) for q in BOTH]
+        softmax_tiles = [{name: kept("gate_%s%d" % (name, q), [P, GATE_TILES, width], F32)
+                          for name, width in (("max", 1), ("diff", E), ("exp", E), ("sum", 1), ("inv", 1),
+                                              ("g", E), ("rest", E))}
+                         for q in BOTH]
+        live = {}
+
+        nc.gpsimd.memset(table_warmup[:], 0.0)
         make_identity(nc, ident32[:])
-        nc.scalar.dma_start(out=vscale[:], in_=v_scale.rearrange("(g p t) a o -> p g (t a o)", p=P, t=4))
-        nc.scalar.dma_start(out=wg_sb[:].rearrange("p g t e -> p g (t e)"), in_=wg.rearrange("(g p t) e -> p g (t e)", p=P, t=4))
-        nc.scalar.activation(out=warm[:, 1:2], in_=warm[:, 0:1], func=ACT.Exp)
+        nc.scalar.dma_start(out=vscale[:], in_=v_scale.rearrange("(g p t) a o -> p g (t a o)", p=P, t=PACK))
+        nc.scalar.dma_start(out=wg_sb[:].rearrange("p g t e -> p g (t e)"),
+                            in_=wg.rearrange("(g p t) e -> p g (t e)", p=P, t=PACK))
+        nc.scalar.activation(out=table_warmup[:, 1:2], in_=table_warmup[:, 0:1], func=ACT.Exp)
         nc.vector.memset(c_rows[:].bitcast(U32), 0)
-        for q in range(batches):
+        for q in BOTH:
             nc.vector.memset(gate_parts[q][:].bitcast(U32), 0)
         nc.vector.tensor_copy(out=ident16[:], in_=ident32[:])
 
-        v_rows = v_bytes.rearrange("(g p t) e r -> g p t (e r)", p=P, t=4)
-        u_rows = u.rearrange("e r d -> (e r) d").rearrange("(h q t i) d -> h t q i d", h=2, t=4, i=4)
+        v_rows = v_bytes.rearrange("(g p t) e r -> g p t (e r)", p=P, t=PACK)
+        u_rows = u.rearrange("e r d -> (e r) d").rearrange("(h q t i) d -> h t q i d", h=2, t=PACK, i=4)
 
         def load_x(j):
-            nc.sync.dma_start(out=x_sb[j], in_=x[j * P:(j + 1) * P, :])
+            nc.sync.dma_start(out=x_all[:, j * D:(j + 1) * D], in_=x[j * P:(j + 1) * P, :])
 
-        nc.sync.dma_start(out=v_raw[0][:, 0:2, :], in_=v_rows[0][:, 0:2, :])
-        nc.sync.dma_start(out=v_raw[0][:, 2:4, :], in_=v_rows[0][:, 2:4, :])
+        for t in (0, 2):
+            nc.sync.dma_start(out=v_raw[0][:, t:t + 2, :], in_=v_rows[0][:, t:t + 2, :])
         load_x(0)
         load_x(1)
         nc.sync.dma_start(out=v_raw[1][:], in_=v_rows[1])
-        for j in range(2, 4):
-            load_x(j)
+        load_x(2)
+        load_x(3)
         for e in range(E):
             nc.sync.dma_start(out=c_rows[4 * e:4 * e + 4, e * R:(e + 1) * R], in_=c[e].partition_broadcast(4))
-        for j in range(4, TILES):
+        for j in range(GATE_TILES, TILES):
             load_x(j)
-        for h in range(2):
-            for t in range(4):
-                nc.sync.dma_start(out=u_raw[h][:, t, :], in_=u_rows[h][t])
+        for rp in BOTH:
+            for t in range(PACK):
+                nc.sync.dma_start(out=u_raw[rp][:, t, :], in_=u_rows[rp][t])
         nc.sync.dma_start(out=b_all[:], in_=b.partition_broadcast(P))
         for j in range(TILES):
             nc.sync.dma_start(out=x0_sb[j][:], in_=x0[j * P:(j + 1) * P, :])
 
-        def copy_on(engine, out_ap, in_ap):
-            if engine == "V":
-                nc.vector.tensor_copy(out=out_ap, in_=in_ap)
-            else:
-                nc.scalar.copy(out=out_ap, in_=in_ap)
-
         def quantize(codes, scales, grouped):
             nc.vector.quantize_mx(out=codes.bitcast(FP8X4), scales=scales, in_=grouped)
 
-        def widen_v(engine, g, h, slots=range(4)):
-            for t in slots:
-                src = v_raw[g][:, t, 512 * h:512 * (h + 1)].bitcast(FP8)
-                if engine == "V":
-                    nc.vector.tensor_scalar(out=v_wide[g, h][:, t, :], in0=src, scalar1=vscale[:, g, t:t + 1],
-                                            scalar2=None, op0=ALU.mult)
-                else:
-                    nc.scalar.activation(out=v_wide[g, h][:, t, :], in_=src, func=ACT.Copy, scale=vscale[:, g, t:t + 1])
+        def v_bytes_of(dp, rp, t):
+            return v_raw[dp][:, t, HALF * rp:HALF * (rp + 1)].bitcast(FP8)
 
-        def group_v(engine, g, h):
-            copy_on(engine, v_grouped[g, h][:].rearrange("p (s q i t) -> p s q t i", s=4, i=4, t=4),
-                    v_wide[g, h][:].rearrange("p t (q s i) -> p s q t i", s=4, i=4))
+        def widen_on_vector(dp):
+            for t in range(PACK):
+                nc.vector.tensor_scalar(out=v_wide[dp, 0][:, t, :], in0=v_bytes_of(dp, 0, t),
+                                        scalar1=vscale[:, dp, t:t + 1], scalar2=None, op0=ALU.mult)
 
-        def quantize_v(g, h):
-            quantize(v_codes[g, h][:], v_scales[g, h][:], v_grouped[g, h][:])
+        def widen_on_scalar(dp, places):
+            for t in places:
+                nc.scalar.activation(out=v_wide[dp, 1][:, t, :], in_=v_bytes_of(dp, 1, t), func=ACT.Copy,
+                                     scale=vscale[:, dp, t:t + 1])
 
-        def group_u(engine, h, s, lo=0, hi=512):
-            copy_on(engine, u_grouped[h, s][:, 4 * lo:4 * hi].rearrange("p (q i t) -> p q t i", i=4, t=4),
-                    u_raw[h][:, :, 512 * s + lo:512 * s + hi].rearrange("p t (q i) -> p q t i", i=4))
+        def group_v(dp, rp):
+            nc.vector.tensor_copy(out=v_grouped[dp, rp][:].rearrange("p (s q i t) -> p s q t i", s=4, i=4, t=PACK),
+                                  in_=v_wide[dp, rp][:].rearrange("p t (q s i) -> p s q t i", s=4, i=4))
 
-        def quantize_u(h, s):
-            quantize(u_codes[h, s][:], u_scales[h, s][:], u_grouped[h, s][:])
+        def quantize_v(dp, rp):
+            quantize(v_codes[dp, rp][:], v_scales[dp, rp][:], v_grouped[dp, rp][:])
 
-        def turn_x(j):
-            bank = shared_bank("xt%d" % j, [P, 4, P], F32)
-            words = x_sb[j].bitcast(F32)
-            for g in range(2):
-                for w in range(2):
-                    nc.tensor.transpose(bank[:, 2 * g + w, :], words[:, 256 * g + w:256 * (g + 1):2], ident32[:])
-            banks["xt", j] = bank
+        def u_views(rp, half, lo, hi):
+            src = u_raw[rp][:, :, HALF * half + lo:HALF * half + hi].rearrange("p t (n i) -> p n t i", i=4)
+            dst = u_grouped[rp, half][:, PACK * lo:PACK * hi].rearrange("p (n i t) -> p n t i", i=4, t=PACK)
+            return dst, src
 
-        def empty_x(j):
-            words = x_grouped[j][:].rearrange("p g n t -> p (g n t)").bitcast(F32)
-            nc.scalar.copy(out=words.rearrange("p (g n w) -> p g n w", g=2, w=2),
-                           in_=banks["xt", j][:].rearrange("p (g w) n -> p g n w", g=2))
+        def group_u_on_vector(rp, half):
+            dst, src = u_views(rp, half, 0, HALF)
+            nc.vector.tensor_copy(out=dst, in_=src)
 
-        def quantize_x(j):
-            quantize(x_codes[j][:], x_scales[j][:], x_grouped[j][:].rearrange("p g n t -> p (g n t)"))
+        def group_u_on_scalar(rp, half, piece):
+            dst, src = u_views(rp, half, HALF // 2 * piece, HALF // 2 * (piece + 1))
+            nc.scalar.copy(out=dst, in_=src)
 
-        def gate_logits(j):
-            q, jj = batch_of[j]
-            if jj == 0:
-                banks["a", q] = psum.tile([P, len(GATE_BATCHES[q]), E], F32, name="logits%d" % q, tag="gc")
-            for g in range(2):
-                for t in range(4):
-                    nc.tensor.matmul(banks["a", q][:, jj, :], lhsT=x_grouped[j][:, g, :, t], rhs=wg_sb[:, g, t, :],
-                                     start=(g == 0 and t == 0), stop=(g == 1 and t == 3))
-
-        def softmax_steps(q):
-            a = banks["a", q]
-            tmp = gate_tmp[q]
-            wide = [P, len(GATE_BATCHES[q]), E]
-            parts = gate_parts[q][:, 0:len(GATE_BATCHES[q]) * GATE_COLS].rearrange("p (j e s) -> p j e s", e=E, s=4)
-            return [
-                lambda: nc.vector.tensor_reduce(out=tmp["max"][:, :, 0], in_=a[:], axis=mybir.AxisListType.X, op=ALU.max),
-                lambda: nc.vector.tensor_tensor(out=tmp["diff"][:], in0=a[:], in1=tmp["max"][:].to_broadcast(wide), op=ALU.subtract),
-                lambda: nc.scalar.activation(out=tmp["exp"][:], in_=tmp["diff"][:], func=ACT.Exp),
-                lambda: nc.vector.tensor_reduce(out=tmp["sum"][:, :, 0], in_=tmp["exp"][:], axis=mybir.AxisListType.X, op=ALU.add),
-                lambda: nc.vector.reciprocal(out=tmp["inv"][:], in_=tmp["sum"][:]),
-                lambda: nc.vector.tensor_tensor(out=tmp["g"][:], in0=tmp["exp"][:], in1=tmp["inv"][:].to_broadcast(wide), op=ALU.mult),
-                lambda: nc.vector.tensor_copy(out=parts[:, :, :, 0], in_=tmp["g"][:]),
-                lambda: nc.vector.tensor_tensor(out=tmp["rest"][:], in0=tmp["g"][:], in1=parts[:, :, :, 0], op=ALU.subtract),
-                lambda: nc.vector.tensor_copy(out=parts[:, :, :, 1], in_=tmp["rest"][:]),
-                lambda: nc.vector.tensor_tensor(out=parts[:, :, :, 2], in0=tmp["rest"][:], in1=parts[:, :, :, 1], op=ALU.subtract),
-            ]
-
-        def turn_gate(q, between=None):
-            bank = shared_bank("gate_t%d" % q, [P, len(GATE_BATCHES[q]), P], BF16)
-            for jj in range(len(GATE_BATCHES[q])):
-                nc.tensor.transpose(bank[:, jj, :], gate_parts[q][:, jj * GATE_COLS:jj * GATE_COLS + P], ident16[:])
-            if between:
-                between()
-            nc.scalar.copy(out=gate_rows[q][:], in_=bank[:])
+        def quantize_u(rp, half):
+            quantize(u_codes[rp, half][:], u_scales[rp, half][:], u_grouped[rp, half][:])
 
         def select_c():
             nc.vector.tensor_copy(out=c_sel[:].rearrange("p h s (q i) -> p h s q i", i=4),
                                   in_=c_rows[:].rearrange("p (h q s i) -> p h s q i", h=2, s=4, i=4))
 
-        def project_down(j, h):
-            bank = psum.tile([P, 4, P], F32, name="p%d%d" % (j, h), tag="p")
-            for s in range(4):
+        def b_onto_partitions():
+            bank = shared_bank("b_bank", [P, D // P, 2], F32)
+            for k in range(D // P):
+                nc.tensor.matmul(bank[:, k, :], lhsT=b_all[:, P * k:P * (k + 1)], rhs=ident16[:, 0:2],
+                                 start=True, stop=True)
+            nc.scalar.copy(out=b_col[:], in_=bank[:])
+
+        def turn_x(j):
+            bank = shared_bank("xt%d" % j, [P, 4, P], F32)
+            words = x_all[:, j * D:(j + 1) * D].bitcast(F32)
+            for dp in BOTH:
+                for w in BOTH:
+                    nc.tensor.transpose(bank[:, 2 * dp + w, :], words[:, 256 * dp + w:256 * (dp + 1):2], ident32[:])
+            live["xt", j] = bank
+
+        def empty_x(j):
+            words = x_grouped[j // 2][:, j % 2].rearrange("p g n t -> p (g n t)").bitcast(F32)
+            nc.scalar.copy(out=words.rearrange("p (g n w) -> p g n w", g=2, w=2),
+                           in_=live["xt", j][:].rearrange("p (g w) n -> p g n w", g=2))
+
+        def quantize_x(m):
+            quantize(x_codes[m][:].rearrange("p j g n -> p (j g n)"), x_scales[m][:].rearrange("p j g n -> p (j g n)"),
+                     x_grouped[m][:].rearrange("p j g n t -> p (j g n t)"))
+
+        def gate_logits(j):
+            q, place = divmod(j, GATE_TILES)
+            if place == 0:
+                live["logits", q] = psum.tile([P, GATE_TILES, E], F32, name="logits%d" % q, tag="gc")
+            for dp in BOTH:
+                for t in range(PACK):
+                    nc.tensor.matmul(live["logits", q][:, place, :], lhsT=x_grouped[j // 2][:, j % 2, dp, :, t],
+                                     rhs=wg_sb[:, dp, t, :], start=(dp == 0 and t == 0),
+                                     stop=(dp == 1 and t == PACK - 1))
+
+        def softmax_steps(q):
+            logits = live["logits", q]
+            s = softmax_tiles[q]
+            wide = [P, GATE_TILES, E]
+            parts = gate_parts[q][:, 0:GATE_TILES * GATE_ROWS].rearrange("p (j e k) -> p j e k", e=E, k=4)
+
+            def subtract_and_exp():
+                nc.vector.tensor_tensor(out=s["diff"][:], in0=logits[:], in1=s["max"][:].to_broadcast(wide),
+                                        op=ALU.subtract)
+                nc.scalar.activation(out=s["exp"][:], in_=s["diff"][:], func=ACT.Exp)
+
+            return [
+                lambda: nc.vector.tensor_reduce(out=s["max"][:, :, 0], in_=logits[:], axis=AXIS_X, op=ALU.max),
+                subtract_and_exp,
+                lambda: nc.vector.tensor_reduce(out=s["sum"][:, :, 0], in_=s["exp"][:], axis=AXIS_X, op=ALU.add),
+                lambda: nc.vector.reciprocal(out=s["inv"][:], in_=s["sum"][:]),
+                lambda: nc.vector.tensor_tensor(out=s["g"][:], in0=s["exp"][:], in1=s["inv"][:].to_broadcast(wide),
+                                                op=ALU.mult),
+                lambda: nc.vector.tensor_copy(out=parts[:, :, :, 0], in_=s["g"][:]),
+                lambda: nc.vector.tensor_tensor(out=s["rest"][:], in0=s["g"][:], in1=parts[:, :, :, 0],
+                                                op=ALU.subtract),
+                lambda: nc.vector.tensor_copy(out=parts[:, :, :, 1], in_=s["rest"][:]),
+                lambda: nc.vector.tensor_tensor(out=parts[:, :, :, 2], in0=s["rest"][:], in1=parts[:, :, :, 1],
+                                                op=ALU.subtract),
+            ]
+
+        def turn_gate(q):
+            bank = shared_bank("gate_t%d" % q, [P, GATE_TILES, P], BF16)
+            for place in range(GATE_TILES):
+                nc.tensor.transpose(bank[:, place, :], gate_parts[q][:, place * GATE_ROWS:place * GATE_ROWS + P],
+                                    ident16[:])
+            nc.scalar.copy(out=gate_rows[q][:], in_=bank[:])
+
+        def project_down(j, rp):
+            bank = psum.tile([P, PACK, P], F32, name="p%d%d" % (j, rp), tag="p")
+            for s in range(PACK):
                 cols = slice(P * s, P * (s + 1))
-                for g in range(2):
-                    nc.tensor.matmul_mx(out=bank[:, s, :], lhsT=v_codes[g, h][:, cols].bitcast(FP8X4),
-                                        lhsT_scale=v_scales[g, h][:, cols],
-                                        rhs=x_codes[j][:, P * g:P * (g + 1)].bitcast(FP8X4),
-                                        rhs_scale=x_scales[j][:, P * g:P * (g + 1)], start=(g == 0), stop=(g == 1))
-            banks["p", j, h] = bank
+                for dp in BOTH:
+                    nc.tensor.matmul_mx(out=bank[:, s, :], lhsT=v_codes[dp, rp][:, cols].bitcast(FP8X4),
+                                        lhsT_scale=v_scales[dp, rp][:, cols],
+                                        rhs=x_codes[j // 2][:, j % 2, dp, :].bitcast(FP8X4),
+                                        rhs_scale=x_scales[j // 2][:, j % 2, dp, :], start=(dp == 0), stop=(dp == 1))
+            live["p", j, rp] = bank
 
-        def tanh_p(j, h):
-            th = work.tile([P, P, 4], F32, name="tanh%d%d" % (j, h), tag="tanh", bufs=6)
-            nc.scalar.activation(out=th[:], in_=banks["p", j, h][:].rearrange("p s n -> p n s"), func=ACT.Tanh)
-            banks["th", j, h] = th
+        def tanh_p(j, rp):
+            tanh = work.tile([P, P, PACK], F32, name="tanh%d%d" % (j, rp), tag="tanh", bufs=6)
+            nc.scalar.activation(out=tanh[:], in_=live["p", j, rp][:].rearrange("p t n -> p n t"), func=ACT.Tanh)
+            live["tanh", j, rp] = tanh
 
-        def gate_times_c(j, h):
-            q, jj = batch_of[j]
-            bank = psum.tile([P, 4, P], F32, name="gc%d%d" % (j, h), tag="gc")
-            for s in range(4):
-                nc.tensor.matmul(bank[:, s, :], lhsT=c_sel[:, h, s, :], rhs=gate_rows[q][:, jj, :], start=True, stop=True)
-            banks["gc", j, h] = bank
+        def tanh_of_projection(j):
+            for rp in BOTH:
+                project_down(j, rp)
+                tanh_p(j, rp)
 
-        def make_h(j, h):
-            if j not in h_grouped:
-                h_grouped[j] = work.tile([P, 2, P, 4], BF16, name="h_grouped%d" % j, tag="h_grouped", bufs=3, align_bytes=64)
-            nc.vector.tensor_tensor(out=h_grouped[j][:, h], in0=banks["th", j, h][:],
-                                    in1=banks["gc", j, h][:].rearrange("p s n -> p n s"), op=ALU.mult)
+        def gate_times_c(j, rp):
+            q, place = divmod(j, GATE_TILES)
+            bank = psum.tile([P, PACK, P], F32, name="gc%d%d" % (j, rp), tag="gc")
+            for s in range(PACK):
+                nc.tensor.matmul(bank[:, s, :], lhsT=c_sel[:, rp, s, :], rhs=gate_rows[q][:, place, :],
+                                 start=True, stop=True)
+            live["gc", j, rp] = bank
+
+        def make_h(j, rp):
+            if rp == 0:
+                live["h", j] = work.tile([P, 2, P, PACK], BF16, name="h%d" % j, tag="h", align_bytes=64)
+            nc.vector.tensor_tensor(out=live["h", j][:, rp], in0=live["tanh", j, rp][:],
+                                    in1=live["gc", j, rp][:].rearrange("p t n -> p n t"), op=ALU.mult)
 
         def quantize_h(j):
-            quantize(h_codes[j][:], h_scales[j][:], h_grouped[j][:].rearrange("p h n t -> p (h n t)"))
+            quantize(h_codes[j][:].rearrange("p h n -> p (h n)"), h_scales[j][:].rearrange("p h n -> p (h n)"),
+                     live["h", j][:].rearrange("p h n t -> p (h n t)"))
 
-        def project_up(j, s):
-            bank = shared_bank("z%d%d" % (j, s), [P, 512], F32)
-            for h in range(2):
-                nc.tensor.matmul_mx(out=bank[:], lhsT=h_codes[j][:, P * h:P * (h + 1)].bitcast(FP8X4),
-                                    lhsT_scale=h_scales[j][:, P * h:P * (h + 1)],
-                                    rhs=u_codes[h, s][:].bitcast(FP8X4), rhs_scale=u_scales[h, s][:],
-                                    start=(h == 0), stop=(h == 1))
-            banks["z", j, s] = bank
+        def cross_half(j, half):
+            return cross[:, j * D + HALF * half:j * D + HALF * (half + 1)]
 
-        def cross_tile(j):
-            return cross[:, j * D:(j + 1) * D]
+        def project_up_plain(j):
+            bank = shared_bank("z%d" % j, [P, HALF], F32)
+            for rp in BOTH:
+                nc.tensor.matmul_mx(out=bank[:], lhsT=h_codes[j][:, rp, :].bitcast(FP8X4),
+                                    lhsT_scale=h_scales[j][:, rp, :], rhs=u_codes[rp, 0][:].bitcast(FP8X4),
+                                    rhs_scale=u_scales[rp, 0][:], start=(rp == 0), stop=(rp == 1))
+            live["z", j] = bank
 
-        def add_b(j, s):
-            cols = slice(512 * s, 512 * (s + 1))
-            nc.vector.tensor_tensor(out=cross_tile(j)[:, cols], in0=banks["z", j, s][:], in1=b_all[:, cols], op=ALU.add)
+        def add_b_plain(j):
+            nc.vector.tensor_tensor(out=cross_half(j, 0), in0=live["z", j][:], in1=b_all[:, 0:HALF], op=ALU.add)
 
-        def times_x0(j, s):
-            cols = slice(512 * s, 512 * (s + 1))
-            nc.vector.tensor_tensor(out=cross_tile(j)[:, cols], in0=cross_tile(j)[:, cols], in1=x0_sb[j][:, cols], op=ALU.mult)
+        def times_x0_plain(j):
+            nc.vector.tensor_tensor(out=cross_half(j, 0), in0=cross_half(j, 0), in1=x0_sb[j][:, 0:HALF], op=ALU.mult)
 
-        def b_columns_mm():
-            bank = shared_bank("b_col_bank", [P, 8, 2], F32)
-            for k in range(8):
-                nc.tensor.matmul(bank[:, k, :], lhsT=b_all[:, P * k:P * (k + 1)], rhs=ident16[:, 0:2], start=True, stop=True)
-            banks["b_col"] = bank
-
-        def b_columns_copy():
-            nc.scalar.copy(out=b_col[:], in_=banks["b_col"][:])
-
-        def project_up_turned(j, s):
-            bank = shared_bank("zt%d%d" % (j, s), [P, 4, P], F32)
+        def project_up_turned(j, half):
+            bank = shared_bank("zt%d%d" % (j, half), [P, 4, P], F32)
             for k in range(4):
                 cols = slice(P * k, P * (k + 1))
-                for h in range(2):
-                    nc.tensor.matmul_mx(out=bank[:, k, :], lhsT=u_codes[h, s][:, cols].bitcast(FP8X4),
-                                        lhsT_scale=u_scales[h, s][:, cols],
-                                        rhs=h_codes[j][:, P * h:P * (h + 1)].bitcast(FP8X4),
-                                        rhs_scale=h_scales[j][:, P * h:P * (h + 1)], start=(h == 0), stop=(h == 1))
-            zt = work.tile([P, 4, P], F32, name="zt_sb%d%d" % (j, s), tag="zt_sb", bufs=3)
+                for rp in BOTH:
+                    nc.tensor.matmul_mx(out=bank[:, k, :], lhsT=u_codes[rp, half][:, cols].bitcast(FP8X4),
+                                        lhsT_scale=u_scales[rp, half][:, cols],
+                                        rhs=h_codes[j][:, rp, :].bitcast(FP8X4), rhs_scale=h_scales[j][:, rp, :],
+                                        start=(rp == 0), stop=(rp == 1))
+            biased = work.tile([P, 4, P], F32, name="biased%d%d" % (j, half), tag="biased", bufs=4)
             for k in range(4):
-                nc.scalar.activation(out=zt[:, k, :], in_=bank[:, k, :], func=ACT.Identity, bias=b_col[:, 4 * s + k, 0:1])
-            banks["zt", j, s] = zt
+                nc.scalar.activation(out=biased[:, k, :], in_=bank[:, k, :], func=ACT.Identity,
+                                     bias=b_col[:, 4 * half + k, 0:1])
+            live["biased", j, half] = biased
 
-        def turn_back(j, s, after=None):
-            bank = shared_bank("zb%d%d" % (j, s), [P, 4, P], F32)
+        def turn_back(j, half):
+            bank = shared_bank("back%d%d" % (j, half), [P, 4, P], F32)
             for k in range(4):
-                nc.tensor.transpose(bank[:, k, :], banks["zt", j, s][:, k, :], ident32[:])
-            banks["zb", j, s] = bank
-            if after:
-                after()
+                nc.tensor.transpose(bank[:, k, :], live["biased", j, half][:, k, :], ident32[:])
+            live["back", j, half] = bank
 
-        def times_x0_turned(j, s):
-            cols = slice(512 * s, 512 * (s + 1))
-            nc.vector.tensor_tensor(out=cross_tile(j)[:, cols], in0=banks["zb", j, s][:].rearrange("p k n -> p (k n)"),
-                                    in1=x0_sb[j][:, cols], op=ALU.mult)
+        def times_x0_turned(j, half):
+            nc.vector.tensor_tensor(out=cross_half(j, half),
+                                    in0=live["back", j, half][:].rearrange("p k n -> p (k n)"),
+                                    in1=x0_sb[j][:, HALF * half:HALF * (half + 1)], op=ALU.mult)
 
-        def add_x(engine, lo, hi):
-            engine.tensor_tensor(out=cross[:, lo:hi], in0=cross[:, lo:hi], in1=x_all[:, lo:hi], op=ALU.add)
+        def add_x_and_store(engine, first, count):
+            cols = slice(HALF * first, HALF * (first + count))
+            engine.tensor_tensor(out=cross[:, cols], in0=cross[:, cols], in1=x_all[:, cols], op=ALU.add)
+            for n in range(first, first + count):
+                j, half = divmod(n, 2)
+                nc.sync.dma_start(out=out[j * P:(j + 1) * P, HALF * half:HALF * (half + 1)], in_=cross_half(j, half))
 
-        def store(lo, hi):
-            j = lo // D
-            nc.sync.dma_start(out=out[j * P:(j + 1) * P, lo - j * D:hi - j * D], in_=cross[:, lo:hi])
-
-        def p_tanh(j, h):
-            project_down(j, h)
-            tanh_p(j, h)
-
-        def x_in(j):
-            turn_x(j)
-            empty_x(j)
+        def weave(steps, between):
+            for step, calls in zip(steps, between):
+                step()
+                for call, *args in calls:
+                    call(*args)
 
         turn_x(0)
         turn_x(1)
-        widen_v("V", 0, 0)
-        widen_v("S", 0, 1)
+        widen_on_vector(0)
+        widen_on_scalar(0, range(PACK))
         empty_x(0)
         empty_x(1)
-        group_v("V", 0, 0)
-        group_v("V", 0, 1)
+        group_v(0, 0)
+        group_v(0, 1)
         gate_logits(0)
         turn_x(2)
         turn_x(3)
         gate_logits(1)
-        widen_v("V", 1, 0)
-        widen_v("S", 1, 1, range(2))
+        widen_on_vector(1)
+        widen_on_scalar(1, (0, 1))
         empty_x(2)
         empty_x(3)
-        widen_v("S", 1, 1, range(2, 4))
+        widen_on_scalar(1, (2, 3))
         turn_x(4)
         gate_logits(2)
         gate_logits(3)
@@ -326,152 +343,85 @@ def tile_dcnmixlowrankcrossexperts_kernel(tc, x0, x, v_bytes, v_scale, wg, c, u,
         turn_x(6)
         turn_x(7)
         quantize_v(0, 0)
-        group_v("V", 1, 0)
+        group_v(1, 0)
         quantize_x(0)
         quantize_v(1, 0)
-        sm = softmax_steps(0)
-        sm[0]()
-        quantize_v(0, 1)
-        sm[1]()
-        empty_x(6)
-        sm[2]()
-        empty_x(7)
-        group_v("V", 1, 1)
-        sm[3]()
-        gate_logits(4)
-        project_down(0, 0)
-        gate_logits(5)
-        group_u("S", 0, 0, 0, 256)
-        tanh_p(0, 0)
-        quantize_x(1)
-        sm[4]()
-        quantize_v(1, 1)
-        sm[5]()
-        select_c()
-        sm[6]()
-        quantize_x(2)
-        sm[7]()
-        quantize_x(3)
-        sm[8]()
-        quantize_x(4)
-        sm[9]()
+
+        weave(softmax_steps(0), [
+            [(quantize_v, 0, 1), (empty_x, 6)],
+            [(empty_x, 7), (group_v, 1, 1)],
+            [(gate_logits, 4), (project_down, 0, 0), (gate_logits, 5), (group_u_on_scalar, 0, 0, 0), (tanh_p, 0, 0),
+             (select_c,)],
+            [(quantize_v, 1, 1)],
+            [(quantize_x, 1)],
+            [(quantize_x, 2)],
+            [(quantize_x, 3)],
+            [],
+            [(group_u_on_vector, 1, 1)],
+        ])
         gate_logits(6)
         gate_logits(7)
-        group_u("S", 0, 0, 256, 512)
-        group_u("S", 1, 0, 0, 256)
-        turn_gate(0)
+        group_u_on_scalar(0, 0, 1)
+        group_u_on_scalar(1, 0, 0)
         project_down(0, 1)
-        gate_times_c(0, 0)
         project_down(1, 0)
-        group_u("S", 1, 0, 256, 512)
         tanh_p(0, 1)
-        sm = softmax_steps(1)
-        quantize_x(5)
-        group_u(U11, 1, 1)
-        sm[0]()
-        quantize_u(0, 0)
-        sm[1]()
-        sm[2]()
-        gate_times_c(0, 1)
-        tanh_p(1, 0)
-        project_down(1, 1)
-        group_u("S", 0, 1, 0, 256)
-        tanh_p(1, 1)
-        group_u("S", 0, 1, 256, 512)
-        quantize_u(1, 1)
-        make_h(0, 0)
-        gate_times_c(1, 0)
-        quantize_u(1, 0)
-        sm[3]()
-        make_h(0, 1)
-        gate_times_c(1, 1)
-        sm[4]()
-        quantize_x(6)
-        sm[5]()
-        quantize_h(0)
-        sm[6]()
-        project_down(2, 0)
-        project_up(0, 0)
-        project_down(2, 1)
-        tanh_p(2, 0)
-        tanh_p(2, 1)
-        make_h(1, 0)
-        sm[7]()
-        quantize_x(7)
-        sm[8]()
-        make_h(1, 1)
-        sm[9]()
-        add_b(0, 0)
-        b_columns_mm()
-        turn_gate(1)
-        b_columns_copy()
-        quantize_u(0, 1)
-        quantize_h(1)
-        times_x0(0, 0)
+        turn_gate(0)
+        gate_times_c(0, 0)
+        group_u_on_scalar(1, 0, 1)
 
-        add_x(nc.gpsimd, 0, 512)
-        store(0, 512)
-        for i in range(1, TILES - 1):
-            make, fetch, done = i + 1, i + 2, i - 1
-            plain = i < TILES - 2
-            gate_times_c(make, 0)
-            if i == 1:
-                gate_times_c(make, 1)
-                p_tanh(fetch, 0)
-                project_up_turned(done, 1)
-                project_up(i, 0)
-                turn_back(done, 1)
-            else:
-                turn_back(done, 1)
-                gate_times_c(make, 1)
-                if plain:
-                    project_up(i, 0)
-                else:
-                    project_up_turned(i, 0)
+        weave(softmax_steps(1), [
+            [(quantize_u, 0, 0)],
+            [(gate_times_c, 0, 1), (project_down, 1, 1), (tanh_p, 1, 0), (group_u_on_scalar, 0, 1, 0), (tanh_p, 1, 1),
+             (group_u_on_scalar, 0, 1, 1), (quantize_u, 1, 1), (make_h, 0, 0), (gate_times_c, 1, 0)],
+            [(quantize_u, 1, 0)],
+            [(project_down, 2, 0), (make_h, 0, 1), (gate_times_c, 1, 1)],
+            [(make_h, 1, 0)],
+            [(b_onto_partitions,), (project_down, 2, 1), (tanh_p, 2, 0), (tanh_p, 2, 1), (quantize_h, 0)],
+            [(make_h, 1, 1)],
+            [(quantize_u, 0, 1)],
+            [(quantize_h, 1)],
+        ])
+
+        for i in range(TILES - 2):
+            gate_times_c(i + 2, 0)
+            if i > 0:
+                turn_back(i - 1, 1)
+            if i + 3 == GATE_TILES:
+                turn_gate(1)
+            gate_times_c(i + 2, 1)
+            project_up_plain(i)
+            make_h(i + 2, 0)
+            if i > 0:
+                times_x0_turned(i - 1, 1)
+            add_b_plain(i)
+            make_h(i + 2, 1)
             project_up_turned(i, 1)
-            make_h(make, 0)
-            if i == 1:
-                make_h(make, 1)
-                add_b(i, 0)
-                times_x0_turned(done, 1)
+            if i + 3 < TILES:
+                tanh_of_projection(i + 3)
+            times_x0_plain(i)
+            quantize_h(i + 2)
+            if i == 0:
+                add_x_and_store(nc.gpsimd, 0, 1)
             else:
-                times_x0_turned(done, 1)
-                if plain:
-                    add_b(i, 0)
-                make_h(make, 1)
-            if fetch < TILES:
-                if i > 1:
-                    p_tanh(fetch, 0)
-                p_tanh(fetch, 1)
-            if i >= 2 and plain:
-                lo = done * D - 512
-                add_x(nc.vector, lo + ADD_G, lo + D)
-                store(lo + 512, lo + D)
-            if plain:
-                times_x0(i, 0)
-            quantize_h(make)
-            lo = i * D - 512
-            share = ADD_G if i < TILES - 3 else (LAST_G if plain else 512)
-            add_x(nc.gpsimd, lo, lo + share)
-            store(lo, lo + 512)
-        done, last = TILES - 2, TILES - 1
-        turn_back(done, 0)
-        turn_back(done, 1)
-        project_up_turned(last, 0)
-        project_up_turned(last, 1)
-        times_x0_turned(done, 0)
-        times_x0_turned(done, 1)
-        lo = (done - 1) * D - 512
-        add_x(nc.vector, lo + LAST_G, lo + D)
-        store(lo + 512, lo + D)
-        add_x(nc.vector, done * D, done * D + 512)
-        store(done * D, done * D + 512)
-        turn_back(last, 0)
-        turn_back(last, 1)
-        add_x(nc.vector, done * D + 512, last * D)
-        store(done * D + 512, last * D)
-        times_x0_turned(last, 0)
-        times_x0_turned(last, 1)
-        for lo, hi in ((0, 512), (512, D)):
-            add_x(nc.vector, last * D + lo, last * D + hi)
-            store(last * D + lo, last * D + hi)
+                add_x_and_store(nc.gpsimd, 2 * i - 1, 2)
+
+        before, last = TILES - 2, TILES - 1
+        for half in BOTH:
+            project_up_turned(before, half)
+        turn_back(before - 1, 1)
+        turn_back(before, 0)
+        times_x0_turned(before - 1, 1)
+        turn_back(before, 1)
+        times_x0_turned(before, 0)
+        for half in BOTH:
+            project_up_turned(last, half)
+        times_x0_turned(before, 1)
+        for half in BOTH:
+            turn_back(last, half)
+        for n in range(2 * before - 1, 2 * last):
+            add_x_and_store(nc.vector, n, 1)
+        for half in BOTH:
+            times_x0_turned(last, half)
+        for half in BOTH:
+            add_x_and_store(nc.vector, 2 * last + half, 1)

from contextlib import ExitStack

import concourse.mybir as mybir
from concourse.masks import make_identity

T, D, E, R = 1024, 1024, 4, 256
FLOPS = 2 * T * D * E * R * 2 + 2 * T * D * E

F32 = mybir.dt.float32
BF16 = mybir.dt.bfloat16
U32 = mybir.dt.uint32
U8 = mybir.dt.uint8
FP8 = mybir.dt.float8_e4m3fn
FP8X4 = mybir.dt.float8_e4m3fn_x4
ALU = mybir.AluOpType
ACT = mybir.ActivationFunctionType
AXIS_X = mybir.AxisListType.X

P = 128
PACK = 4
HALF = 512
TILES = T // P
GATE_TILES = 4
GATE_ROWS = 16
BOTH = (0, 1)
QUARTERS = ((0, 0), (0, 1), (1, 0), (1, 1))


def tile_dcnmixlowrankcrossexperts_kernel(tc, x0, x, v_bytes, v_scale, wg, c, u, b, out):
    nc = tc.nc
    with ExitStack() as ctx:
        keep = ctx.enter_context(tc.tile_pool(name="keep", bufs=1))
        work = ctx.enter_context(tc.tile_pool(name="work", bufs=3))
        psum = ctx.enter_context(tc.psum_pool(name="psum", bufs=2))
        ctx.enter_context(tc.manual_schedule())

        def kept(name, shape, dtype):
            return keep.tile(shape, dtype, name=name, align_bytes=64)

        def quarters(name, shape, dtype):
            return {key: kept("%s%d%d" % (name, key[0], key[1]), shape, dtype) for key in QUARTERS}

        def shared_bank(name, shape, dtype):
            return psum.tile(shape, dtype, name=name, tag="shared", bufs=4)

        ident32 = kept("ident32", [P, P], F32)
        ident16 = kept("ident16", [P, P], BF16)
        table_warmup = kept("table_warmup", [P, 2], F32)
        vscale = kept("vscale", [P, 2, PACK], F32)
        wg_sb = kept("wg_sb", [P, 2, PACK, E], BF16)
        c_rows = kept("c_rows", [P, E * R], BF16)
        c_sel = kept("c_sel", [P, 2, PACK, P], BF16)
        b_all = kept("b_all", [P, D], BF16)
        b_col = kept("b_col", [P, D // P, 2], F32)
        v_raw = [kept("v_raw%d" % dp, [P, PACK, E * R], U8) for dp in BOTH]
        v_wide = quarters("v_wide", [P, PACK, HALF], BF16)
        v_grouped = quarters("v_grouped", [P, PACK * HALF], BF16)
        v_codes = quarters("v_codes", [P, HALF], U32)
        v_scales = quarters("v_scales", [P, HALF], U8)
        u_raw = [kept("u_raw%d" % rp, [P, PACK, D], BF16) for rp in BOTH]
        u_grouped = quarters("u_grouped", [P, PACK * HALF], BF16)
        u_codes = quarters("u_codes", [P, HALF], U32)
        u_scales = quarters("u_scales", [P, HALF], U8)
        x_all = kept("x_all", [P, TILES * D], BF16)
        cross = kept("cross", [P, TILES * D], F32)
        x0_sb = [kept("x0_sb%d" % j, [P, D], BF16) for j in range(TILES)]
        x_grouped = [kept("x_grouped%d" % m, [P, 2, 2, P, PACK], BF16) for m in range(TILES // 2)]
        x_codes = [kept("x_codes%d" % m, [P, 2, 2, P], U32) for m in range(TILES // 2)]
        x_scales = [kept("x_scales%d" % m, [P, 2, 2, P], U8) for m in range(TILES // 2)]
        h_codes = [kept("h_codes%d" % j, [P, 2, P], U32) for j in range(TILES)]
        h_scales = [kept("h_scales%d" % j, [P, 2, P], U8) for j in range(TILES)]
        gate_parts = [kept("gate_parts%d" % q, [P, (GATE_TILES - 1) * GATE_ROWS + P], BF16) for q in BOTH]
        gate_rows = [kept("gate_rows%d" % q, [P, GATE_TILES, P], BF16) for q in BOTH]
        softmax_tiles = [{name: kept("gate_%s%d" % (name, q), [P, GATE_TILES, width], F32)
                          for name, width in (("max", 1), ("diff", E), ("exp", E), ("sum", 1), ("inv", 1),
                                              ("g", E), ("rest", E))}
                         for q in BOTH]
        live = {}

        nc.gpsimd.memset(table_warmup[:], 0.0)
        make_identity(nc, ident32[:])
        nc.scalar.dma_start(out=vscale[:], in_=v_scale.rearrange("(g p t) a o -> p g (t a o)", p=P, t=PACK))
        nc.scalar.dma_start(out=wg_sb[:].rearrange("p g t e -> p g (t e)"),
                            in_=wg.rearrange("(g p t) e -> p g (t e)", p=P, t=PACK))
        nc.scalar.activation(out=table_warmup[:, 1:2], in_=table_warmup[:, 0:1], func=ACT.Exp)
        nc.vector.memset(c_rows[:].bitcast(U32), 0)
        for q in BOTH:
            nc.vector.memset(gate_parts[q][:].bitcast(U32), 0)
        nc.vector.tensor_copy(out=ident16[:], in_=ident32[:])

        v_rows = v_bytes.rearrange("(g p t) e r -> g p t (e r)", p=P, t=PACK)
        u_rows = u.rearrange("e r d -> (e r) d").rearrange("(h q t i) d -> h t q i d", h=2, t=PACK, i=4)

        def load_x(j):
            nc.sync.dma_start(out=x_all[:, j * D:(j + 1) * D], in_=x[j * P:(j + 1) * P, :])

        for t in (0, 2):
            nc.sync.dma_start(out=v_raw[0][:, t:t + 2, :], in_=v_rows[0][:, t:t + 2, :])
        load_x(0)
        load_x(1)
        nc.sync.dma_start(out=v_raw[1][:], in_=v_rows[1])
        load_x(2)
        load_x(3)
        for e in range(E):
            nc.sync.dma_start(out=c_rows[4 * e:4 * e + 4, e * R:(e + 1) * R], in_=c[e].partition_broadcast(4))
        for j in range(GATE_TILES, TILES):
            load_x(j)
        for rp in BOTH:
            for t in range(PACK):
                nc.sync.dma_start(out=u_raw[rp][:, t, :], in_=u_rows[rp][t])
        nc.sync.dma_start(out=b_all[:], in_=b.partition_broadcast(P))
        for j in range(TILES):
            nc.sync.dma_start(out=x0_sb[j][:], in_=x0[j * P:(j + 1) * P, :])

        def quantize(codes, scales, grouped):
            nc.vector.quantize_mx(out=codes.bitcast(FP8X4), scales=scales, in_=grouped)

        def v_bytes_of(dp, rp, t):
            return v_raw[dp][:, t, HALF * rp:HALF * (rp + 1)].bitcast(FP8)

        def widen_on_vector(dp):
            for t in range(PACK):
                nc.vector.tensor_scalar(out=v_wide[dp, 0][:, t, :], in0=v_bytes_of(dp, 0, t),
                                        scalar1=vscale[:, dp, t:t + 1], scalar2=None, op0=ALU.mult)

        def widen_on_scalar(dp, places):
            for t in places:
                nc.scalar.activation(out=v_wide[dp, 1][:, t, :], in_=v_bytes_of(dp, 1, t), func=ACT.Copy,
                                     scale=vscale[:, dp, t:t + 1])

        def group_v(dp, rp):
            nc.vector.tensor_copy(out=v_grouped[dp, rp][:].rearrange("p (s q i t) -> p s q t i", s=4, i=4, t=PACK),
                                  in_=v_wide[dp, rp][:].rearrange("p t (q s i) -> p s q t i", s=4, i=4))

        def quantize_v(dp, rp):
            quantize(v_codes[dp, rp][:], v_scales[dp, rp][:], v_grouped[dp, rp][:])

        def u_views(rp, half, lo, hi):
            src = u_raw[rp][:, :, HALF * half + lo:HALF * half + hi].rearrange("p t (n i) -> p n t i", i=4)
            dst = u_grouped[rp, half][:, PACK * lo:PACK * hi].rearrange("p (n i t) -> p n t i", i=4, t=PACK)
            return dst, src

        def group_u_on_vector(rp, half):
            dst, src = u_views(rp, half, 0, HALF)
            nc.vector.tensor_copy(out=dst, in_=src)

        def group_u_on_scalar(rp, half, piece):
            dst, src = u_views(rp, half, HALF // 2 * piece, HALF // 2 * (piece + 1))
            nc.scalar.copy(out=dst, in_=src)

        def quantize_u(rp, half):
            quantize(u_codes[rp, half][:], u_scales[rp, half][:], u_grouped[rp, half][:])

        def select_c():
            nc.vector.tensor_copy(out=c_sel[:].rearrange("p h s (q i) -> p h s q i", i=4),
                                  in_=c_rows[:].rearrange("p (h q s i) -> p h s q i", h=2, s=4, i=4))

        def b_onto_partitions():
            bank = shared_bank("b_bank", [P, D // P, 2], F32)
            for k in range(D // P):
                nc.tensor.matmul(bank[:, k, :], lhsT=b_all[:, P * k:P * (k + 1)], rhs=ident16[:, 0:2],
                                 start=True, stop=True)
            nc.scalar.copy(out=b_col[:], in_=bank[:])

        def turn_x(j):
            bank = shared_bank("xt%d" % j, [P, 4, P], F32)
            words = x_all[:, j * D:(j + 1) * D].bitcast(F32)
            for dp in BOTH:
                for w in BOTH:
                    nc.tensor.transpose(bank[:, 2 * dp + w, :], words[:, 256 * dp + w:256 * (dp + 1):2], ident32[:])
            live["xt", j] = bank

        def empty_x(j):
            words = x_grouped[j // 2][:, j % 2].rearrange("p g n t -> p (g n t)").bitcast(F32)
            nc.scalar.copy(out=words.rearrange("p (g n w) -> p g n w", g=2, w=2),
                           in_=live["xt", j][:].rearrange("p (g w) n -> p g n w", g=2))

        def quantize_x(m):
            quantize(x_codes[m][:].rearrange("p j g n -> p (j g n)"), x_scales[m][:].rearrange("p j g n -> p (j g n)"),
                     x_grouped[m][:].rearrange("p j g n t -> p (j g n t)"))

        def gate_logits(j):
            q, place = divmod(j, GATE_TILES)
            if place == 0:
                live["logits", q] = psum.tile([P, GATE_TILES, E], F32, name="logits%d" % q, tag="gc")
            for dp in BOTH:
                for t in range(PACK):
                    nc.tensor.matmul(live["logits", q][:, place, :], lhsT=x_grouped[j // 2][:, j % 2, dp, :, t],
                                     rhs=wg_sb[:, dp, t, :], start=(dp == 0 and t == 0),
                                     stop=(dp == 1 and t == PACK - 1))

        def softmax_steps(q):
            logits = live["logits", q]
            s = softmax_tiles[q]
            wide = [P, GATE_TILES, E]
            parts = gate_parts[q][:, 0:GATE_TILES * GATE_ROWS].rearrange("p (j e k) -> p j e k", e=E, k=4)

            def subtract_and_exp():
                nc.vector.tensor_tensor(out=s["diff"][:], in0=logits[:], in1=s["max"][:].to_broadcast(wide),
                                        op=ALU.subtract)
                nc.scalar.activation(out=s["exp"][:], in_=s["diff"][:], func=ACT.Exp)

            return [
                lambda: nc.vector.tensor_reduce(out=s["max"][:, :, 0], in_=logits[:], axis=AXIS_X, op=ALU.max),
                subtract_and_exp,
                lambda: nc.vector.tensor_reduce(out=s["sum"][:, :, 0], in_=s["exp"][:], axis=AXIS_X, op=ALU.add),
                lambda: nc.vector.reciprocal(out=s["inv"][:], in_=s["sum"][:]),
                lambda: nc.vector.tensor_tensor(out=s["g"][:], in0=s["exp"][:], in1=s["inv"][:].to_broadcast(wide),
                                                op=ALU.mult),
                lambda: nc.vector.tensor_copy(out=parts[:, :, :, 0], in_=s["g"][:]),
                lambda: nc.vector.tensor_tensor(out=s["rest"][:], in0=s["g"][:], in1=parts[:, :, :, 0],
                                                op=ALU.subtract),
                lambda: nc.vector.tensor_copy(out=parts[:, :, :, 1], in_=s["rest"][:]),
                lambda: nc.vector.tensor_tensor(out=parts[:, :, :, 2], in0=s["rest"][:], in1=parts[:, :, :, 1],
                                                op=ALU.subtract),
            ]

        def turn_gate(q):
            bank = shared_bank("gate_t%d" % q, [P, GATE_TILES, P], BF16)
            for place in range(GATE_TILES):
                nc.tensor.transpose(bank[:, place, :], gate_parts[q][:, place * GATE_ROWS:place * GATE_ROWS + P],
                                    ident16[:])
            nc.scalar.copy(out=gate_rows[q][:], in_=bank[:])

        def project_down(j, rp):
            bank = psum.tile([P, PACK, P], F32, name="p%d%d" % (j, rp), tag="p")
            for s in range(PACK):
                cols = slice(P * s, P * (s + 1))
                for dp in BOTH:
                    nc.tensor.matmul_mx(out=bank[:, s, :], lhsT=v_codes[dp, rp][:, cols].bitcast(FP8X4),
                                        lhsT_scale=v_scales[dp, rp][:, cols],
                                        rhs=x_codes[j // 2][:, j % 2, dp, :].bitcast(FP8X4),
                                        rhs_scale=x_scales[j // 2][:, j % 2, dp, :], start=(dp == 0), stop=(dp == 1))
            live["p", j, rp] = bank

        def tanh_p(j, rp):
            tanh = work.tile([P, P, PACK], F32, name="tanh%d%d" % (j, rp), tag="tanh", bufs=6)
            nc.scalar.activation(out=tanh[:], in_=live["p", j, rp][:].rearrange("p t n -> p n t"), func=ACT.Tanh)
            live["tanh", j, rp] = tanh

        def tanh_of_projection(j):
            for rp in BOTH:
                project_down(j, rp)
                tanh_p(j, rp)

        def gate_times_c(j, rp):
            q, place = divmod(j, GATE_TILES)
            bank = psum.tile([P, PACK, P], F32, name="gc%d%d" % (j, rp), tag="gc")
            for s in range(PACK):
                nc.tensor.matmul(bank[:, s, :], lhsT=c_sel[:, rp, s, :], rhs=gate_rows[q][:, place, :],
                                 start=True, stop=True)
            live["gc", j, rp] = bank

        def make_h(j, rp):
            if rp == 0:
                live["h", j] = work.tile([P, 2, P, PACK], BF16, name="h%d" % j, tag="h", align_bytes=64)
            nc.vector.tensor_tensor(out=live["h", j][:, rp], in0=live["tanh", j, rp][:],
                                    in1=live["gc", j, rp][:].rearrange("p t n -> p n t"), op=ALU.mult)

        def quantize_h(j):
            quantize(h_codes[j][:].rearrange("p h n -> p (h n)"), h_scales[j][:].rearrange("p h n -> p (h n)"),
                     live["h", j][:].rearrange("p h n t -> p (h n t)"))

        def cross_half(j, half):
            return cross[:, j * D + HALF * half:j * D + HALF * (half + 1)]

        def project_up_plain(j):
            bank = shared_bank("z%d" % j, [P, HALF], F32)
            for rp in BOTH:
                nc.tensor.matmul_mx(out=bank[:], lhsT=h_codes[j][:, rp, :].bitcast(FP8X4),
                                    lhsT_scale=h_scales[j][:, rp, :], rhs=u_codes[rp, 0][:].bitcast(FP8X4),
                                    rhs_scale=u_scales[rp, 0][:], start=(rp == 0), stop=(rp == 1))
            live["z", j] = bank

        def add_b_plain(j):
            nc.vector.tensor_tensor(out=cross_half(j, 0), in0=live["z", j][:], in1=b_all[:, 0:HALF], op=ALU.add)

        def times_x0_plain(j):
            nc.vector.tensor_tensor(out=cross_half(j, 0), in0=cross_half(j, 0), in1=x0_sb[j][:, 0:HALF], op=ALU.mult)

        def project_up_turned(j, half):
            bank = shared_bank("zt%d%d" % (j, half), [P, 4, P], F32)
            for k in range(4):
                cols = slice(P * k, P * (k + 1))
                for rp in BOTH:
                    nc.tensor.matmul_mx(out=bank[:, k, :], lhsT=u_codes[rp, half][:, cols].bitcast(FP8X4),
                                        lhsT_scale=u_scales[rp, half][:, cols],
                                        rhs=h_codes[j][:, rp, :].bitcast(FP8X4), rhs_scale=h_scales[j][:, rp, :],
                                        start=(rp == 0), stop=(rp == 1))
            biased = work.tile([P, 4, P], F32, name="biased%d%d" % (j, half), tag="biased", bufs=4)
            for k in range(4):
                nc.scalar.activation(out=biased[:, k, :], in_=bank[:, k, :], func=ACT.Identity,
                                     bias=b_col[:, 4 * half + k, 0:1])
            live["biased", j, half] = biased

        def turn_back(j, half):
            bank = shared_bank("back%d%d" % (j, half), [P, 4, P], F32)
            for k in range(4):
                nc.tensor.transpose(bank[:, k, :], live["biased", j, half][:, k, :], ident32[:])
            live["back", j, half] = bank

        def times_x0_turned(j, half):
            nc.vector.tensor_tensor(out=cross_half(j, half),
                                    in0=live["back", j, half][:].rearrange("p k n -> p (k n)"),
                                    in1=x0_sb[j][:, HALF * half:HALF * (half + 1)], op=ALU.mult)

        def add_x_and_store(engine, first, count):
            cols = slice(HALF * first, HALF * (first + count))
            engine.tensor_tensor(out=cross[:, cols], in0=cross[:, cols], in1=x_all[:, cols], op=ALU.add)
            for n in range(first, first + count):
                j, half = divmod(n, 2)
                nc.sync.dma_start(out=out[j * P:(j + 1) * P, HALF * half:HALF * (half + 1)], in_=cross_half(j, half))

        def weave(steps, between):
            for step, calls in zip(steps, between):
                step()
                for call, *args in calls:
                    call(*args)

        turn_x(0)
        turn_x(1)
        widen_on_vector(0)
        widen_on_scalar(0, range(PACK))
        empty_x(0)
        empty_x(1)
        group_v(0, 0)
        group_v(0, 1)
        gate_logits(0)
        turn_x(2)
        turn_x(3)
        gate_logits(1)
        widen_on_vector(1)
        widen_on_scalar(1, (0, 1))
        empty_x(2)
        empty_x(3)
        widen_on_scalar(1, (2, 3))
        turn_x(4)
        gate_logits(2)
        gate_logits(3)
        turn_x(5)
        empty_x(4)
        empty_x(5)
        turn_x(6)
        turn_x(7)
        quantize_v(0, 0)
        group_v(1, 0)
        quantize_x(0)
        quantize_v(1, 0)

        weave(softmax_steps(0), [
            [(quantize_v, 0, 1), (empty_x, 6)],
            [(empty_x, 7), (group_v, 1, 1)],
            [(gate_logits, 4), (project_down, 0, 0), (gate_logits, 5), (group_u_on_scalar, 0, 0, 0), (tanh_p, 0, 0),
             (select_c,)],
            [(quantize_v, 1, 1)],
            [(quantize_x, 1)],
            [(quantize_x, 2)],
            [(quantize_x, 3)],
            [],
            [(group_u_on_vector, 1, 1)],
        ])
        gate_logits(6)
        gate_logits(7)
        group_u_on_scalar(0, 0, 1)
        group_u_on_scalar(1, 0, 0)
        project_down(0, 1)
        project_down(1, 0)
        tanh_p(0, 1)
        turn_gate(0)
        gate_times_c(0, 0)
        group_u_on_scalar(1, 0, 1)

        weave(softmax_steps(1), [
            [(quantize_u, 0, 0)],
            [(gate_times_c, 0, 1), (project_down, 1, 1), (tanh_p, 1, 0), (group_u_on_scalar, 0, 1, 0), (tanh_p, 1, 1),
             (group_u_on_scalar, 0, 1, 1), (quantize_u, 1, 1), (make_h, 0, 0), (gate_times_c, 1, 0)],
            [(quantize_u, 1, 0)],
            [(project_down, 2, 0), (make_h, 0, 1), (gate_times_c, 1, 1)],
            [(make_h, 1, 0)],
            [(b_onto_partitions,), (project_down, 2, 1), (tanh_p, 2, 0), (tanh_p, 2, 1), (quantize_h, 0)],
            [(make_h, 1, 1)],
            [(quantize_u, 0, 1)],
            [(quantize_h, 1)],
        ])

        for i in range(TILES - 2):
            gate_times_c(i + 2, 0)
            if i > 0:
                turn_back(i - 1, 1)
            if i + 3 == GATE_TILES:
                turn_gate(1)
            gate_times_c(i + 2, 1)
            project_up_plain(i)
            make_h(i + 2, 0)
            if i > 0:
                times_x0_turned(i - 1, 1)
            add_b_plain(i)
            make_h(i + 2, 1)
            project_up_turned(i, 1)
            if i + 3 < TILES:
                tanh_of_projection(i + 3)
            times_x0_plain(i)
            quantize_h(i + 2)
            if i == 0:
                add_x_and_store(nc.gpsimd, 0, 1)
            else:
                add_x_and_store(nc.gpsimd, 2 * i - 1, 2)

        before, last = TILES - 2, TILES - 1
        for half in BOTH:
            project_up_turned(before, half)
        turn_back(before - 1, 1)
        turn_back(before, 0)
        times_x0_turned(before - 1, 1)
        turn_back(before, 1)
        times_x0_turned(before, 0)
        for half in BOTH:
            project_up_turned(last, half)
        times_x0_turned(before, 1)
        for half in BOTH:
            turn_back(last, half)
        for n in range(2 * before - 1, 2 * last):
            add_x_and_store(nc.vector, n, 1)
        for half in BOTH:
            times_x0_turned(last, half)
        for half in BOTH:
            add_x_and_store(nc.vector, 2 * last + half, 1)
